import numpy as np
import ml_dtypes


def mxq(x, axis, fmt="e4m3"):
    dtype, down = {"e4m3": (ml_dtypes.float8_e4m3fn, 7), "e5m2": (ml_dtypes.float8_e5m2, 14)}[fmt]
    v = np.moveaxis(np.asarray(x, np.float32).astype(ml_dtypes.bfloat16).astype(np.float64), axis, -1)
    blocks = v.reshape(v.shape[:-1] + (-1, 32))
    amax = np.abs(blocks).max(-1, keepdims=True)
    byte = np.maximum(np.where(amax > 0, np.frexp(amax)[1] - 1 + 127, 0) - down, 1)
    scale = np.exp2(byte - 127.0)
    codes = (blocks / scale).astype(np.float32).astype(dtype).astype(np.float64)
    return np.moveaxis((codes * scale).reshape(v.shape), -1, axis)


WIDE = False


def mx_kscale(k):
    if not WIDE:
        return np.ones(k)
    levels = np.array([10, -10, 5, -5, 0])
    if k % 512:
        return np.exp2(np.random.permutation(np.resize(levels, k // 32))).repeat(32)
    a = np.empty((k // 512, 16))
    for p in range(k // 512):
        a[p, :8] = np.random.permutation(np.resize(levels, 8))
        for g in range(8):
            far = levels[np.abs(levels - a[p, g]) >= 10]
            a[p, g + 8] = far[np.random.randint(len(far))]
    return np.exp2(a.ravel()).repeat(32)


def f64(x):
    return np.asarray(x).astype(np.float64)


def striped(idx):
    return np.tile(idx.reshape(-1, 16).T, (8, 1)).astype(np.uint16)


def unstriped(offs):
    return offs[:16].T.reshape(-1).astype(np.int64)


E2M1 = np.array([0.0, 0.5, 1.0, 1.5, 2.0, 3.0, 4.0, 6.0, -0.0, -0.5, -1.0, -1.5, -2.0, -3.0, -4.0, -6.0])


def pack_weight(w, fmt):
    k, n = w.shape
    w = f64(np.asarray(w, np.float32).astype(ml_dtypes.bfloat16)).reshape(k // 32, 32, n)
    amax = np.abs(w).max(1)
    if fmt == "e4m3":
        byte = np.frexp(amax)[1] - 1 + 127 - 7
    else:
        mant, ex = np.frexp(amax / 6.0)
        byte = np.where(mant > 0.5, ex, ex - 1) + 127
    byte = np.clip(np.where(amax > 0, byte, 1), 1, 254)
    scaled = (w * np.exp2(127.0 - byte)[:, None, :]).reshape(k, n).astype(np.float32)
    by_word = np.ascontiguousarray(scaled.reshape(k // 512, 128, 4, n).transpose(0, 1, 3, 2))
    if fmt == "e4m3":
        words = by_word.astype(ml_dtypes.float8_e4m3fn).view(np.uint8)
    else:
        c = by_word.astype(ml_dtypes.float4_e2m1fn).view(np.uint8) & 0xF
        words = (c[..., 0::2] | (c[..., 1::2] << 4)).reshape(k // 512, 128, 2 * n)
    return np.ascontiguousarray(words), np.ascontiguousarray(byte.astype(np.uint8).reshape(k // 512, 16, n))


def unpack_weight(words, scales, fmt):
    g, _, n = scales.shape
    words = np.ascontiguousarray(words).reshape(g, 128, n, -1)
    if fmt == "e4m3":
        vals = words.view(ml_dtypes.float8_e4m3fn).astype(np.float64)
    else:
        nib = np.empty((g, 128, n, 4), np.uint8)
        nib[..., 0::2] = words & 0xF
        nib[..., 1::2] = words >> 4
        vals = E2M1[nib]
    vals = vals * np.repeat(np.exp2(scales.astype(np.float64) - 127.0), 8, axis=1)[..., None]
    return vals.transpose(0, 1, 3, 2).reshape(g * 512, n)


K, M, T, S = 1024, 1024, 4096, 1536


def setup_inputs():
    n = np.random.standard_normal
    s = mx_kscale(K)[:, None]
    w = n((K, M)) / np.sqrt(K) / s
    v = pack_weight(n((K, T)) * s, "e4m3")
    p_w4 = pack_weight(w[512:], "e2m1")
    return {
        "tab_words": v[0],
        "tab_scales": v[1],
        "w8": (w[:512]).astype(np.float32),
        "w4_words": p_w4[0],
        "w4_scales": p_w4[1],
        "ts": np.tile(np.exp(0.5 * n(T)), (128, 1)).astype(np.float32),
        "b": (0.3 * n(1024)).astype(np.float32),
        "offs": striped(np.random.permutation(T)[:S]),
    }


def reference(tab_words, tab_scales, w8, w4_words, w4_scales, ts, b, offs):
    tab_ = unpack_weight(tab_words, tab_scales, "e4m3")[:, unstriped(offs)]
    w8_ = mxq(f64(w8), 0, "e4m3")
    w4_ = unpack_weight(w4_words, w4_scales, "e2m1")
    y = w8_.T @ tab_[:512] + w4_.T @ tab_[512:]
    y = y * f64(ts)[0][unstriped(offs)]
    return y + f64(b)[:, None]

@@ -1,0 +1,182 @@
+from contextlib import ExitStack
+
+import concourse.mybir as mybir
+from concourse.masks import make_identity
+
+K, M, T, S = 1024, 1024, 4096, 1536
+FLOPS = 2 * K * M * S
+
+F32 = mybir.dt.float32
+BF16 = mybir.dt.bfloat16
+I32 = mybir.dt.int32
+U32 = mybir.dt.uint32
+U16 = mybir.dt.uint16
+U8 = mybir.dt.uint8
+FP8X4 = mybir.dt.float8_e4m3fn_x4
+FP4X4 = mybir.dt.float4_e2m1fn_x4
+MULT = mybir.AluOpType.mult
+ADD = mybir.AluOpType.add
+IDENTITY = mybir.ActivationFunctionType.Identity
+
+P = 128
+PACK = 4
+BANK = 512
+SLICES = S // BANK
+LIST_COLS = BANK // 16
+HALF = M // 2
+CAST = 256
+PLANE0 = 12
+
+
+def tile_list_tabts_bias_kernel(
+    tc, tab_words, tab_scales, w8, w4_words, w4_scales, ts, b, offs, out
+):
+    nc = tc.nc
+    with ExitStack() as ctx:
+        keep = ctx.enter_context(tc.tile_pool(name="keep", bufs=1))
+        ring = ctx.enter_context(tc.tile_pool(name="ring", bufs=6))
+        psum = ctx.enter_context(tc.psum_pool(name="psum", bufs=8))
+
+        offsets = keep.tile([P, S // 16], U16, name="offsets")
+        ts_cols = keep.tile([P, T // P], F32, name="ts_cols", tag="slot_a", align_bytes=64)
+        ts_window = keep.tile([P, T], F32, name="ts_window", tag="slot_b", align_bytes=64)
+        scale_window = keep.tile([P, T], U8, name="scale_window", tag="slot_c", align_bytes=64)
+        word_window = [keep.tile([P, T], I32, name="word_window%d" % a) for a in range(2)]
+        w8_raw = [keep.tile([P, PACK, HALF], F32, name="w8_raw%d" % h) for h in range(2)]
+        w8_bf16 = {}
+        w8_codes = [keep.tile([P, HALF], U32, name="w8_codes%d" % h, align_bytes=64) for h in range(2)]
+        w8_plane = [keep.tile([P, HALF], U8, name="w8_plane%d" % h, align_bytes=64) for h in range(2)]
+        w4_codes = keep.tile([P, 2 * M], U8, name="w4_codes", align_bytes=64)
+        w4_plane = keep.tile([P, M // 4], I32, name="w4_plane", align_bytes=64)
+        bias = keep.tile([P, M // P], F32, name="bias")
+        identity = keep.tile([P, P], F32, name="identity")
+        picked_scales = keep.tile([P, S], U8, name="picked_scales", align_bytes=64)
+        picked_words = {}
+        picked_ts = [keep.tile([P, BANK], F32, name="picked_ts%d" % s) for s in range(SLICES)]
+
+        make_identity(nc, identity[:])
+        nc.vector.memset(w4_plane[:], 0)
+
+        scale_rows = tab_scales.rearrange("a q t -> (a q) t").bitcast(I32)
+        planes = scale_window[:].bitcast(I32)
+
+        def load_scale_rows(queue, first_partition, count, first_row):
+            queue.dma_start(
+                planes[first_partition : first_partition + count, :], scale_rows[first_row : first_row + count, :]
+            )
+
+        def load_words(a):
+            nc.sync.dma_start(word_window[a][:], tab_words[a].rearrange("p t i -> p (t i)").bitcast(I32))
+
+        def load_w8(h):
+            rows = w8.rearrange("(p i) n -> p i n", i=PACK)
+            nc.sync.dma_start(w8_raw[h][:], rows[:, :, h * HALF : (h + 1) * HALF])
+
+        nc.sync.dma_start(offsets[:], offs)
+        load_scale_rows(nc.scalar, 0, 12, 16)
+        load_scale_rows(nc.scalar, 100, 28, 4)
+        load_scale_rows(nc.sync, 12, 32, 0)
+        load_scale_rows(nc.sync, 68, 32, 0)
+        load_scale_rows(nc.sync, 44, 16, 4)
+        load_scale_rows(nc.sync, 60, 8, 20)
+        nc.gpsimd.dma_start(ts_cols[:], ts[0].rearrange("(p c) -> p c", p=P))
+        load_words(0)
+        load_w8(0)
+        nc.sync.dma_start(w4_codes[:].bitcast(I32), w4_words[0].bitcast(I32))
+        for q in range(4):
+            nc.sync.dma_start(
+                w4_plane[32 * q : 32 * q + 4, :], w4_scales[0].bitcast(I32)[4 * q : 4 * q + 4, :]
+            )
+        load_words(1)
+        with nc.allow_non_contiguous_dma(reason="one bias value for each partition"):
+            nc.sync.dma_start(bias[:], b.rearrange("(c p) -> p c", p=P))
+        load_w8(1)
+
+        window_lines = ts_window[:].rearrange("q (p c) -> q p c", p=P)
+        for g in range(T // BANK):
+            spread = psum.tile([P, BANK], F32, name="bank")
+            for i in range(PACK):
+                c = PACK * g + i
+                nc.tensor.transpose(
+                    spread[:, i * P : (i + 1) * P], ts_cols[:, c : c + 1].to_broadcast([P, P]), identity[:]
+                )
+            nc.scalar.copy(
+                window_lines[:, :, PACK * g : PACK * (g + 1)], spread[:].rearrange("q (i p) -> q p i", i=PACK)
+            )
+
+        def list_slice(s):
+            return offsets[:, s * LIST_COLS : (s + 1) * LIST_COLS]
+
+        def gather_words(a, s):
+            nc.vector.tensor_copy(picked_words[a][:, s * BANK : (s + 1) * BANK], word_window[a][:].bitcast(U32).indirect(list_slice(s)))
+
+        def round_w8(h):
+            for c0 in range(0, HALF, CAST):
+                nc.scalar.copy(
+                    w8_bf16[h][:, c0 : c0 + CAST, :].rearrange("p (c u) i -> p c i u", u=4),
+                    w8_raw[h][:, :, c0 : c0 + CAST].rearrange("p i (c u) -> p c i u", u=4),
+                )
+
+        def quantize_w8(h):
+            nc.vector.quantize_mx(
+                out=w8_codes[h][:].bitcast(FP8X4),
+                scales=w8_plane[h][:],
+                in_=w8_bf16[h][:].rearrange("p n i -> p (n i)"),
+            )
+
+        def output_tiles(s, h):
+            cols = slice(s * BANK, (s + 1) * BANK)
+            for c in range(HALF // P):
+                n0 = h * HALF + c * P
+                acc = psum.tile([P, BANK], F32, name="bank")
+                nc.tensor.matmul_mx(
+                    out=acc[:],
+                    lhsT=w8_codes[h][:, c * P : (c + 1) * P].bitcast(FP8X4),
+                    lhsT_scale=w8_plane[h][:, c * P : (c + 1) * P],
+                    rhs=picked_words[0][:, cols].bitcast(FP8X4),
+                    rhs_scale=picked_scales[PLANE0:P, cols],
+                    start=True,
+                    stop=False,
+                )
+                nc.tensor.matmul_mx(
+                    out=acc[:],
+                    lhsT=w4_codes[:, 2 * n0 : 2 * (n0 + P)].bitcast(FP4X4),
+                    lhsT_scale=w4_plane[:].bitcast(U8)[:, n0 : n0 + P],
+                    rhs=picked_words[1][:, cols].bitcast(FP8X4),
+                    rhs_scale=picked_scales[:, cols],
+                    start=False,
+                    stop=True,
+                )
+                scaled = ring.tile([P, BANK], F32, name="scaled")
+                nc.vector.tensor_tensor(scaled[:], acc[:], picked_ts[s][:], MULT)
+                result = ring.tile([P, BANK], F32, name="result", bufs=8)
+                bias_col = bias[:, n0 // P : n0 // P + 1]
+                if (s, h) == (0, 0):
+                    nc.gpsimd.tensor_scalar(result[:], scaled[:], 1.0, bias_col, MULT, ADD)
+                else:
+                    nc.scalar.activation(result[:], scaled[:], IDENTITY, bias=bias_col)
+                nc.sync.dma_start(out[n0 : n0 + P, cols], result[:])
+
+        nc.vector.tensor_copy(picked_scales[:], scale_window[:].indirect(offsets[:]))
+        picked_words[0] = keep.tile([P, S], U32, name="picked_words0", tag="slot_c", align_bytes=64)
+        for s in range(SLICES):
+            gather_words(0, s)
+        w8_bf16[0] = keep.tile([P, HALF, PACK], BF16, name="w8_bf16_0", tag="slot_a", align_bytes=64)
+        round_w8(0)
+        for s in range(SLICES):
+            if s == SLICES - 1:
+                quantize_w8(0)
+            nc.vector.tensor_copy(picked_ts[s][:], ts_window[:].indirect(list_slice(s)))
+        picked_words[1] = keep.tile([P, S], U32, name="picked_words1", tag="slot_b", align_bytes=64)
+        gather_words(1, 0)
+        output_tiles(0, 0)
+        gather_words(1, 1)
+        w8_bf16[1] = keep.tile([P, HALF, PACK], BF16, name="w8_bf16_1", tag="slot_a", align_bytes=64)
+        round_w8(1)
+        output_tiles(1, 0)
+        quantize_w8(1)
+        output_tiles(0, 1)
+        output_tiles(1, 1)
+        gather_words(1, 2)
+        output_tiles(2, 0)
+        output_tiles(2, 1)

@@ -26,6 +26,9 @@ LIST_COLS = BANK // 16
 HALF = M // 2
 CAST = 256
 PLANE0 = 12
+TILES = [(s, 4 * h + c) for s, h in ((0, 0), (1, 0), (0, 1), (1, 1), (2, 0), (2, 1)) for c in range(4)]
+POOL_MULT = ()
+POOL_BIAS = ()
 
 
 def tile_list_tabts_bias_kernel(
@@ -35,27 +38,33 @@ def tile_list_tabts_bias_kernel(
     with ExitStack() as ctx:
         keep = ctx.enter_context(tc.tile_pool(name="keep", bufs=1))
         ring = ctx.enter_context(tc.tile_pool(name="ring", bufs=6))
+        shared = ctx.enter_context(tc.tile_pool(name="shared", bufs=1))
         psum = ctx.enter_context(tc.psum_pool(name="psum", bufs=8))
 
+        def slot_tile(k, shape, dtype, name):
+            return shared.tile(shape, dtype, name=name, offset=k * BANK * 4, align_bytes=64)
+
         offsets = keep.tile([P, S // 16], U16, name="offsets")
-        ts_cols = keep.tile([P, T // P], F32, name="ts_cols", tag="slot_a", align_bytes=64)
-        ts_window = keep.tile([P, T], F32, name="ts_window", tag="slot_b", align_bytes=64)
-        scale_window = keep.tile([P, T], U8, name="scale_window", tag="slot_c", align_bytes=64)
-        word_window = [keep.tile([P, T], I32, name="word_window%d" % a) for a in range(2)]
+        ts_cols = slot_tile(0, [P, T // P], F32, "ts_cols")
+        bias_rows = slot_tile(1, [P, P], F32, "bias_rows")
+        ts_window = keep.tile([P, T], F32, name="ts_window")
+        scale_window = keep.tile([P, T], U8, name="scale_window", tag="scale_window", align_bytes=64)
+        word_window = [
+            keep.tile([P, T], I32, name="word_window%d" % a, tag="word_window%d" % a, align_bytes=64) for a in range(2)
+        ]
         w8_raw = [keep.tile([P, PACK, HALF], F32, name="w8_raw%d" % h) for h in range(2)]
-        w8_bf16 = {}
-        w8_codes = [keep.tile([P, HALF], U32, name="w8_codes%d" % h, align_bytes=64) for h in range(2)]
-        w8_plane = [keep.tile([P, HALF], U8, name="w8_plane%d" % h, align_bytes=64) for h in range(2)]
+        w8_codes = keep.tile([P, M], U32, name="w8_codes", align_bytes=64)
+        w8_plane = keep.tile([P, M], U8, name="w8_plane", align_bytes=64)
         w4_codes = keep.tile([P, 2 * M], U8, name="w4_codes", align_bytes=64)
         w4_plane = keep.tile([P, M // 4], I32, name="w4_plane", align_bytes=64)
         bias = keep.tile([P, M // P], F32, name="bias")
         identity = keep.tile([P, P], F32, name="identity")
-        picked_scales = keep.tile([P, S], U8, name="picked_scales", align_bytes=64)
-        picked_words = {}
-        picked_ts = [keep.tile([P, BANK], F32, name="picked_ts%d" % s) for s in range(SLICES)]
+        w8_bf16, picked_scales, picked_words, picked_ts = {}, {}, {}, {}
 
         make_identity(nc, identity[:])
         nc.vector.memset(w4_plane[:], 0)
+        nc.gpsimd.memset(bias_rows[:], 0.0)
+        nc.gpsimd.dma_start(bias_rows[0 : M // P, :], b.rearrange("(c x) -> c x", x=P))
 
         scale_rows = tab_scales.rearrange("a q t -> (a q) t").bitcast(I32)
         planes = scale_window[:].bitcast(I32)
@@ -65,31 +74,26 @@ def tile_list_tabts_bias_kernel(
                 planes[first_partition : first_partition + count, :], scale_rows[first_row : first_row + count, :]
             )
 
-        def load_words(a):
-            nc.sync.dma_start(word_window[a][:], tab_words[a].rearrange("p t i -> p (t i)").bitcast(I32))
+        def load_words(queue, a):
+            queue.dma_start(word_window[a][:], tab_words[a].rearrange("p t i -> p (t i)").bitcast(I32))
 
         def load_w8(h):
             rows = w8.rearrange("(p i) n -> p i n", i=PACK)
             nc.sync.dma_start(w8_raw[h][:], rows[:, :, h * HALF : (h + 1) * HALF])
 
         nc.sync.dma_start(offsets[:], offs)
-        load_scale_rows(nc.scalar, 0, 12, 16)
-        load_scale_rows(nc.scalar, 100, 28, 4)
+        nc.sync.dma_start(ts_cols[:], ts[0].rearrange("(p c) -> p c", p=P))
+        load_words(nc.sync, 0)
+        load_scale_rows(nc.sync, 0, 12, 16)
+        load_scale_rows(nc.sync, 100, 28, 4)
         load_scale_rows(nc.sync, 12, 32, 0)
         load_scale_rows(nc.sync, 68, 32, 0)
-        load_scale_rows(nc.sync, 44, 16, 4)
-        load_scale_rows(nc.sync, 60, 8, 20)
-        nc.gpsimd.dma_start(ts_cols[:], ts[0].rearrange("(p c) -> p c", p=P))
-        load_words(0)
+        load_scale_rows(nc.sync, 44, 24, 4)
         load_w8(0)
         nc.sync.dma_start(w4_codes[:].bitcast(I32), w4_words[0].bitcast(I32))
         for q in range(4):
-            nc.sync.dma_start(
-                w4_plane[32 * q : 32 * q + 4, :], w4_scales[0].bitcast(I32)[4 * q : 4 * q + 4, :]
-            )
-        load_words(1)
-        with nc.allow_non_contiguous_dma(reason="one bias value for each partition"):
-            nc.sync.dma_start(bias[:], b.rearrange("(c p) -> p c", p=P))
+            nc.sync.dma_start(w4_plane[32 * q : 32 * q + 4, :], w4_scales[0].bitcast(I32)[4 * q : 4 * q + 4, :])
+        load_words(nc.sync, 1)
         load_w8(1)
 
         window_lines = ts_window[:].rearrange("q (p c) -> q p c", p=P)
@@ -104,79 +108,107 @@ def tile_list_tabts_bias_kernel(
                 window_lines[:, :, PACK * g : PACK * (g + 1)], spread[:].rearrange("q (i p) -> q p i", i=PACK)
             )
 
+        bias_bank = psum.tile([P, BANK], F32, name="bank")
+        nc.tensor.transpose(bias_bank[:, 0:P], bias_rows[:], identity[:])
+        nc.scalar.copy(bias[:], bias_bank[:, 0 : M // P])
+
         def list_slice(s):
             return offsets[:, s * LIST_COLS : (s + 1) * LIST_COLS]
 
-        def gather_words(a, s):
-            nc.vector.tensor_copy(picked_words[a][:, s * BANK : (s + 1) * BANK], word_window[a][:].bitcast(U32).indirect(list_slice(s)))
+        def gather_words(a, s, tile):
+            picked_words[a, s] = tile
+            nc.vector.tensor_copy(tile[:], word_window[a][:].bitcast(U32).indirect(list_slice(s)))
 
-        def round_w8(h):
-            for c0 in range(0, HALF, CAST):
-                nc.scalar.copy(
-                    w8_bf16[h][:, c0 : c0 + CAST, :].rearrange("p (c u) i -> p c i u", u=4),
-                    w8_raw[h][:, :, c0 : c0 + CAST].rearrange("p i (c u) -> p c i u", u=4),
-                )
+        def gather_scales(s, tile):
+            picked_scales[s] = tile
+            nc.vector.tensor_copy(tile[:], scale_window[:].indirect(list_slice(s)))
 
-        def quantize_w8(h):
-            nc.vector.quantize_mx(
-                out=w8_codes[h][:].bitcast(FP8X4),
-                scales=w8_plane[h][:],
-                in_=w8_bf16[h][:].rearrange("p n i -> p (n i)"),
+        def gather_ts(s, tile):
+            picked_ts[s] = tile
+            nc.vector.tensor_copy(tile[:], ts_window[:].indirect(list_slice(s)))
+
+        def round_w8(k, slot):
+            w8_bf16[k] = slot_tile(slot, [P, CAST, PACK], BF16, "w8_bf16_%d" % k)
+            first = k % 2 * CAST
+            nc.scalar.copy(
+                w8_bf16[k][:].rearrange("p (c u) i -> p c i u", u=4),
+                w8_raw[k // 2][:, :, first : first + CAST].rearrange("p i (c u) -> p c i u", u=4),
             )
 
-        def output_tiles(s, h):
-            cols = slice(s * BANK, (s + 1) * BANK)
-            for c in range(HALF // P):
-                n0 = h * HALF + c * P
-                acc = psum.tile([P, BANK], F32, name="bank")
-                nc.tensor.matmul_mx(
-                    out=acc[:],
-                    lhsT=w8_codes[h][:, c * P : (c + 1) * P].bitcast(FP8X4),
-                    lhsT_scale=w8_plane[h][:, c * P : (c + 1) * P],
-                    rhs=picked_words[0][:, cols].bitcast(FP8X4),
-                    rhs_scale=picked_scales[PLANE0:P, cols],
-                    start=True,
-                    stop=False,
-                )
-                nc.tensor.matmul_mx(
-                    out=acc[:],
-                    lhsT=w4_codes[:, 2 * n0 : 2 * (n0 + P)].bitcast(FP4X4),
-                    lhsT_scale=w4_plane[:].bitcast(U8)[:, n0 : n0 + P],
-                    rhs=picked_words[1][:, cols].bitcast(FP8X4),
-                    rhs_scale=picked_scales[:, cols],
-                    start=False,
-                    stop=True,
-                )
-                scaled = ring.tile([P, BANK], F32, name="scaled")
-                nc.vector.tensor_tensor(scaled[:], acc[:], picked_ts[s][:], MULT)
-                result = ring.tile([P, BANK], F32, name="result", bufs=8)
-                bias_col = bias[:, n0 // P : n0 // P + 1]
-                if (s, h) == (0, 0):
-                    nc.gpsimd.tensor_scalar(result[:], scaled[:], 1.0, bias_col, MULT, ADD)
-                else:
-                    nc.scalar.activation(result[:], scaled[:], IDENTITY, bias=bias_col)
-                nc.sync.dma_start(out[n0 : n0 + P, cols], result[:])
+        def quantize_w8(k):
+            nc.vector.quantize_mx(
+                out=w8_codes[:, k * CAST : (k + 1) * CAST].bitcast(FP8X4),
+                scales=w8_plane[:, k * CAST : (k + 1) * CAST],
+                in_=w8_bf16[k][:].rearrange("p n i -> p (n i)"),
+            )
 
-        nc.vector.tensor_copy(picked_scales[:], scale_window[:].indirect(offsets[:]))
-        picked_words[0] = keep.tile([P, S], U32, name="picked_words0", tag="slot_c", align_bytes=64)
+        def output_tile(t, slot=None):
+            s, c = TILES[t]
+            rows = slice(c * P, (c + 1) * P)
+            acc = psum.tile([P, BANK], F32, name="bank")
+            nc.tensor.matmul_mx(
+                out=acc[:],
+                lhsT=w8_codes[:, rows].bitcast(FP8X4),
+                lhsT_scale=w8_plane[:, rows],
+                rhs=picked_words[0, s][:].bitcast(FP8X4),
+                rhs_scale=picked_scales[s][PLANE0:P, :],
+                start=True,
+                stop=False,
+            )
+            nc.tensor.matmul_mx(
+                out=acc[:],
+                lhsT=w4_codes[:, 2 * c * P : 2 * (c + 1) * P].bitcast(FP4X4),
+                lhsT_scale=w4_plane[:].bitcast(U8)[:, rows],
+                rhs=picked_words[1, s][:].bitcast(FP8X4),
+                rhs_scale=picked_scales[s][:],
+                start=False,
+                stop=True,
+            )
+            if slot is None:
+                scaled = ring.tile([P, BANK], F32, name="scaled")
+            else:
+                scaled = slot_tile(slot, [P, BANK], F32, "scaled%d" % t)
+            if t in POOL_MULT:
+                plain = ring.tile([P, BANK], F32, name="plain", bufs=3)
+                nc.scalar.copy(plain[:], acc[:])
+                nc.gpsimd.tensor_tensor(scaled[:], plain[:], picked_ts[s][:], MULT)
+            else:
+                nc.vector.tensor_tensor(scaled[:], acc[:], picked_ts[s][:], MULT)
+            result = ring.tile([P, BANK], F32, name="result", bufs=8)
+            if t in POOL_BIAS:
+                nc.gpsimd.tensor_scalar(result[:], scaled[:], 1.0, bias[:, c : c + 1], MULT, ADD)
+            else:
+                nc.scalar.activation(result[:], scaled[:], IDENTITY, bias=bias[:, c : c + 1])
+            nc.sync.dma_start(out[rows, s * BANK : (s + 1) * BANK], result[:])
+
         for s in range(SLICES):
-            gather_words(0, s)
-        w8_bf16[0] = keep.tile([P, HALF, PACK], BF16, name="w8_bf16_0", tag="slot_a", align_bytes=64)
-        round_w8(0)
-        for s in range(SLICES):
-            if s == SLICES - 1:
-                quantize_w8(0)
-            nc.vector.tensor_copy(picked_ts[s][:], ts_window[:].indirect(list_slice(s)))
-        picked_words[1] = keep.tile([P, S], U32, name="picked_words1", tag="slot_b", align_bytes=64)
-        gather_words(1, 0)
-        output_tiles(0, 0)
-        gather_words(1, 1)
-        w8_bf16[1] = keep.tile([P, HALF, PACK], BF16, name="w8_bf16_1", tag="slot_a", align_bytes=64)
-        round_w8(1)
-        output_tiles(1, 0)
+            gather_words(0, s, keep.tile([P, BANK], U32, name="picked_words0%d" % s, align_bytes=64))
+        round_w8(0, 0)
+        round_w8(1, 1)
+        gather_scales(0, keep.tile([P, BANK], U8, name="picked_scales0", tag="word_window0", align_bytes=64))
+        quantize_w8(0)
+        gather_scales(1, slot_tile(0, [P, BANK], U8, "picked_scales1"))
         quantize_w8(1)
-        output_tiles(0, 1)
-        output_tiles(1, 1)
-        gather_words(1, 2)
-        output_tiles(2, 0)
-        output_tiles(2, 1)
+        gather_scales(2, slot_tile(1, [P, BANK], U8, "picked_scales2"))
+        gather_ts(0, keep.tile([P, BANK], F32, name="picked_ts0"))
+        gather_words(1, 0, keep.tile([P, BANK], U32, name="picked_words10", tag="scale_window", align_bytes=64))
+        output_tile(0, 2)
+        output_tile(1, 3)
+        output_tile(2, 4)
+        gather_words(1, 1, slot_tile(2, [P, BANK], U32, "picked_words11"))
+        output_tile(3)
+        gather_ts(1, slot_tile(3, [P, BANK], F32, "picked_ts1"))
+        round_w8(2, 4)
+        output_tile(4, 5)
+        output_tile(5)
+        quantize_w8(2)
+        round_w8(3, 5)
+        output_tile(6)
+        output_tile(7)
+        quantize_w8(3)
+        for t in range(8, 24):
+            output_tile(t, {10: 6, 13: 7}.get(t))
+            if t == 12:
+                gather_words(1, 2, slot_tile(6, [P, BANK], U32, "picked_words12"))
+            if t == 14:
+                gather_ts(2, slot_tile(7, [P, BANK], F32, "picked_ts2"))

@@ -24,11 +24,27 @@ BANK = 512
 SLICES = S // BANK
 LIST_COLS = BANK // 16
 HALF = M // 2
-CAST = 256
+ROW_TILES = M // P
+LINE = 4
+QUADRANT = 32
+
 PLANE0 = 12
+SCALE_RUNS = ((0, 12, 16), (100, 28, 4), (12, 32, 0), (68, 32, 0), (44, 24, 4))
+
 TILES = [(s, 4 * h + c) for s, h in ((0, 0), (1, 0), (0, 1), (1, 1), (2, 0), (2, 1)) for c in range(4)]
-POOL_MULT = ()
-POOL_BIAS = ()
+POOL_TILES = [(0, c) for c in range(0, ROW_TILES, 2)]
+LAST_TILE_PIECES = 2
+
+SLOT_BYTES = 4 * BANK
+W8_BF16_SLOT = (0, 2)
+W8_RAW_SLOT = (4, 8)
+TS_COLS_OFFSET = W8_BF16_SLOT[1] * SLOT_BYTES - 64
+WORDS2_GATHER_AT, WORDS2_SLOT = 7, 13
+TS2_GATHER_AT, TS2_SLOT = 13, 12
+SCALED_SLOT = {WORDS2_GATHER_AT - 1: WORDS2_SLOT, TS2_GATHER_AT - 1: TS2_SLOT}
+FIRST_TILE_OF_SLICE1 = 4
+SCALED_BUFS = 10
+PLAIN_BUFS = len(POOL_TILES)
 
 
 def tile_list_tabts_bias_kernel(
@@ -37,121 +53,110 @@ def tile_list_tabts_bias_kernel(
     nc = tc.nc
     with ExitStack() as ctx:
         keep = ctx.enter_context(tc.tile_pool(name="keep", bufs=1))
-        ring = ctx.enter_context(tc.tile_pool(name="ring", bufs=6))
+        ring = ctx.enter_context(tc.tile_pool(name="ring", bufs=1))
         shared = ctx.enter_context(tc.tile_pool(name="shared", bufs=1))
         psum = ctx.enter_context(tc.psum_pool(name="psum", bufs=8))
 
-        def slot_tile(k, shape, dtype, name):
-            return shared.tile(shape, dtype, name=name, offset=k * BANK * 4, align_bytes=64)
+        def slot_tile(slot, shape, dtype, name):
+            return shared.tile(shape, dtype, name=name, offset=slot * SLOT_BYTES, align_bytes=64)
 
         offsets = keep.tile([P, S // 16], U16, name="offsets")
-        ts_cols = slot_tile(0, [P, T // P], F32, "ts_cols")
-        bias_rows = slot_tile(1, [P, P], F32, "bias_rows")
-        ts_window = keep.tile([P, T], F32, name="ts_window")
-        scale_window = keep.tile([P, T], U8, name="scale_window", tag="scale_window", align_bytes=64)
+        ts_cols = shared.tile([P, T // P], F32, name="ts_cols", offset=TS_COLS_OFFSET, align_bytes=64)
+        bias_rows = keep.tile([P, P], F32, name="bias_rows")
+        ts_window = keep.tile([P, T], F32, name="ts_window", align_bytes=64)
+        scale_window = keep.tile([P, T], U8, name="scale_window", align_bytes=64)
         word_window = [
             keep.tile([P, T], I32, name="word_window%d" % a, tag="word_window%d" % a, align_bytes=64) for a in range(2)
         ]
-        w8_raw = [keep.tile([P, PACK, HALF], F32, name="w8_raw%d" % h) for h in range(2)]
-        w8_codes = keep.tile([P, M], U32, name="w8_codes", align_bytes=64)
+        w8_raw = [slot_tile(W8_RAW_SLOT[h], [P, PACK, HALF], F32, "w8_raw%d" % h) for h in range(2)]
+        w8_codes = [keep.tile([P, HALF], U32, name="w8_codes%d" % h, align_bytes=64) for h in range(2)]
         w8_plane = keep.tile([P, M], U8, name="w8_plane", align_bytes=64)
         w4_codes = keep.tile([P, 2 * M], U8, name="w4_codes", align_bytes=64)
         w4_plane = keep.tile([P, M // 4], I32, name="w4_plane", align_bytes=64)
-        bias = keep.tile([P, M // P], F32, name="bias")
+        bias = keep.tile([P, ROW_TILES], F32, name="bias")
         identity = keep.tile([P, P], F32, name="identity")
-        w8_bf16, picked_scales, picked_words, picked_ts = {}, {}, {}, {}
+        results = [keep.tile([P, S], F32, name="result%d" % c) for c in range(ROW_TILES)]
+        w8_bf16, picked_words1, picked_ts = {}, {}, {}
 
         make_identity(nc, identity[:])
+        nc.vector.memset(bias_rows[:], 0.0)
         nc.vector.memset(w4_plane[:], 0)
-        nc.gpsimd.memset(bias_rows[:], 0.0)
-        nc.gpsimd.dma_start(bias_rows[0 : M // P, :], b.rearrange("(c x) -> c x", x=P))
 
-        scale_rows = tab_scales.rearrange("a q t -> (a q) t").bitcast(I32)
-        planes = scale_window[:].bitcast(I32)
-
-        def load_scale_rows(queue, first_partition, count, first_row):
-            queue.dma_start(
-                planes[first_partition : first_partition + count, :], scale_rows[first_row : first_row + count, :]
-            )
-
-        def load_words(queue, a):
-            queue.dma_start(word_window[a][:], tab_words[a].rearrange("p t i -> p (t i)").bitcast(I32))
-
-        def load_w8(h):
-            rows = w8.rearrange("(p i) n -> p i n", i=PACK)
-            nc.sync.dma_start(w8_raw[h][:], rows[:, :, h * HALF : (h + 1) * HALF])
+        def load_words(a):
+            nc.sync.dma_start(word_window[a][:], tab_words[a].rearrange("p t i -> p (t i)").bitcast(I32))
 
         nc.sync.dma_start(offsets[:], offs)
         nc.sync.dma_start(ts_cols[:], ts[0].rearrange("(p c) -> p c", p=P))
-        load_words(nc.sync, 0)
-        load_scale_rows(nc.sync, 0, 12, 16)
-        load_scale_rows(nc.sync, 100, 28, 4)
-        load_scale_rows(nc.sync, 12, 32, 0)
-        load_scale_rows(nc.sync, 68, 32, 0)
-        load_scale_rows(nc.sync, 44, 24, 4)
-        load_w8(0)
+        load_words(0)
+        scale_rows = tab_scales.rearrange("a q t -> (a q) t").bitcast(I32)
+        for partition, count, row in SCALE_RUNS:
+            nc.sync.dma_start(
+                scale_window[:].bitcast(I32)[partition : partition + count, :], scale_rows[row : row + count, :]
+            )
+        nc.sync.dma_start(bias_rows[0:ROW_TILES, :], b.rearrange("(c x) -> c x", x=P))
+        w8_by_partition = w8.rearrange("(p i) n -> p i n", i=PACK)
+        for h in range(2):
+            nc.sync.dma_start(w8_raw[h][:], w8_by_partition[:, :, h * HALF : (h + 1) * HALF])
         nc.sync.dma_start(w4_codes[:].bitcast(I32), w4_words[0].bitcast(I32))
-        for q in range(4):
-            nc.sync.dma_start(w4_plane[32 * q : 32 * q + 4, :], w4_scales[0].bitcast(I32)[4 * q : 4 * q + 4, :])
-        load_words(nc.sync, 1)
-        load_w8(1)
+        for q in range(P // QUADRANT):
+            nc.sync.dma_start(
+                w4_plane[QUADRANT * q : QUADRANT * q + 4, :], w4_scales[0].bitcast(I32)[4 * q : 4 * q + 4, :]
+            )
+        load_words(1)
 
         window_lines = ts_window[:].rearrange("q (p c) -> q p c", p=P)
         for g in range(T // BANK):
             spread = psum.tile([P, BANK], F32, name="bank")
-            for i in range(PACK):
-                c = PACK * g + i
+            for i in range(LINE):
+                c = LINE * g + i
                 nc.tensor.transpose(
                     spread[:, i * P : (i + 1) * P], ts_cols[:, c : c + 1].to_broadcast([P, P]), identity[:]
                 )
             nc.scalar.copy(
-                window_lines[:, :, PACK * g : PACK * (g + 1)], spread[:].rearrange("q (i p) -> q p i", i=PACK)
+                window_lines[:, :, LINE * g : LINE * (g + 1)], spread[:].rearrange("q (i p) -> q p i", i=LINE)
             )
 
         bias_bank = psum.tile([P, BANK], F32, name="bank")
         nc.tensor.transpose(bias_bank[:, 0:P], bias_rows[:], identity[:])
-        nc.scalar.copy(bias[:], bias_bank[:, 0 : M // P])
+        nc.scalar.copy(bias[:], bias_bank[:, 0:ROW_TILES])
 
         def list_slice(s):
             return offsets[:, s * LIST_COLS : (s + 1) * LIST_COLS]
 
-        def gather_words(a, s, tile):
-            picked_words[a, s] = tile
-            nc.vector.tensor_copy(tile[:], word_window[a][:].bitcast(U32).indirect(list_slice(s)))
+        def gather_words1(s, slot):
+            picked_words1[s] = slot_tile(slot, [P, BANK], U32, "picked_words1_%d" % s)
+            nc.vector.tensor_copy(picked_words1[s][:], word_window[1][:].bitcast(U32).indirect(list_slice(s)))
 
-        def gather_scales(s, tile):
-            picked_scales[s] = tile
-            nc.vector.tensor_copy(tile[:], scale_window[:].indirect(list_slice(s)))
+        def gather_ts(s, slot):
+            picked_ts[s] = slot_tile(slot, [P, BANK], F32, "picked_ts%d" % s)
+            nc.vector.tensor_copy(picked_ts[s][:], ts_window[:].indirect(list_slice(s)))
 
-        def gather_ts(s, tile):
-            picked_ts[s] = tile
-            nc.vector.tensor_copy(tile[:], ts_window[:].indirect(list_slice(s)))
-
-        def round_w8(k, slot):
-            w8_bf16[k] = slot_tile(slot, [P, CAST, PACK], BF16, "w8_bf16_%d" % k)
-            first = k % 2 * CAST
+        def round_w8(h):
+            w8_bf16[h] = slot_tile(W8_BF16_SLOT[h], [P, HALF, PACK], BF16, "w8_bf16_%d" % h)
             nc.scalar.copy(
-                w8_bf16[k][:].rearrange("p (c u) i -> p c i u", u=4),
-                w8_raw[k // 2][:, :, first : first + CAST].rearrange("p i (c u) -> p c i u", u=4),
+                w8_bf16[h][:].rearrange("p (c u) i -> p c i u", u=LINE),
+                w8_raw[h][:].rearrange("p i (c u) -> p c i u", u=LINE),
             )
 
-        def quantize_w8(k):
+        def quantize_w8(h):
             nc.vector.quantize_mx(
-                out=w8_codes[:, k * CAST : (k + 1) * CAST].bitcast(FP8X4),
-                scales=w8_plane[:, k * CAST : (k + 1) * CAST],
-                in_=w8_bf16[k][:].rearrange("p n i -> p (n i)"),
+                out=w8_codes[h][:].bitcast(FP8X4),
+                scales=w8_plane[:, h * HALF : (h + 1) * HALF],
+                in_=w8_bf16[h][:].rearrange("p n i -> p (n i)"),
             )
 
-        def output_tile(t, slot=None):
+        def output_tile(t):
             s, c = TILES[t]
             rows = slice(c * P, (c + 1) * P)
+            entries = slice(s * BANK, (s + 1) * BANK)
+            h, first = divmod(c * P, HALF)
             acc = psum.tile([P, BANK], F32, name="bank")
             nc.tensor.matmul_mx(
                 out=acc[:],
-                lhsT=w8_codes[:, rows].bitcast(FP8X4),
+                lhsT=w8_codes[h][:, first : first + P].bitcast(FP8X4),
                 lhsT_scale=w8_plane[:, rows],
-                rhs=picked_words[0, s][:].bitcast(FP8X4),
-                rhs_scale=picked_scales[s][PLANE0:P, :],
+                rhs=picked_words0[:, entries].bitcast(FP8X4),
+                rhs_scale=picked_scales[PLANE0:P, entries],
                 start=True,
                 stop=False,
             )
@@ -159,56 +164,49 @@ def tile_list_tabts_bias_kernel(
                 out=acc[:],
                 lhsT=w4_codes[:, 2 * c * P : 2 * (c + 1) * P].bitcast(FP4X4),
                 lhsT_scale=w4_plane[:].bitcast(U8)[:, rows],
-                rhs=picked_words[1, s][:].bitcast(FP8X4),
-                rhs_scale=picked_scales[s][:],
+                rhs=picked_words1[s][:].bitcast(FP8X4),
+                rhs_scale=picked_scales[:, entries],
                 start=False,
                 stop=True,
             )
-            if slot is None:
-                scaled = ring.tile([P, BANK], F32, name="scaled")
-            else:
-                scaled = slot_tile(slot, [P, BANK], F32, "scaled%d" % t)
-            if t in POOL_MULT:
-                plain = ring.tile([P, BANK], F32, name="plain", bufs=3)
+            bias_column = bias[:, c : c + 1]
+            if (s, c) in POOL_TILES:
+                scaled = ring.tile([P, BANK], F32, name="scaled_pool")
+                plain = ring.tile([P, BANK], F32, name="plain", bufs=PLAIN_BUFS)
                 nc.scalar.copy(plain[:], acc[:])
                 nc.gpsimd.tensor_tensor(scaled[:], plain[:], picked_ts[s][:], MULT)
+                nc.gpsimd.tensor_scalar(results[c][:, entries], scaled[:], 1.0, bias_column, MULT, ADD)
+                return
+            if t in SCALED_SLOT:
+                scaled = slot_tile(SCALED_SLOT[t], [P, BANK], F32, "scaled%d" % t)
             else:
-                nc.vector.tensor_tensor(scaled[:], acc[:], picked_ts[s][:], MULT)
-            result = ring.tile([P, BANK], F32, name="result", bufs=8)
-            if t in POOL_BIAS:
-                nc.gpsimd.tensor_scalar(result[:], scaled[:], 1.0, bias[:, c : c + 1], MULT, ADD)
-            else:
-                nc.scalar.activation(result[:], scaled[:], IDENTITY, bias=bias[:, c : c + 1])
-            nc.sync.dma_start(out[rows, s * BANK : (s + 1) * BANK], result[:])
+                scaled = ring.tile([P, BANK], F32, name="scaled", bufs=SCALED_BUFS)
+            width = BANK // (LAST_TILE_PIECES if t == len(TILES) - 1 else 1)
+            for start in range(0, BANK, width):
+                part = slice(start, start + width)
+                cols = slice(s * BANK + start, s * BANK + start + width)
+                nc.vector.tensor_tensor(scaled[:, part], acc[:, part], picked_ts[s][:, part], MULT)
+                nc.scalar.activation(results[c][:, cols], scaled[:, part], IDENTITY, bias=bias_column)
+                if (s - 1, c) in POOL_TILES:
+                    cols = slice(cols.start - BANK, cols.stop)
+                nc.sync.dma_start(out[rows, cols], results[c][:, cols])
 
-        for s in range(SLICES):
-            gather_words(0, s, keep.tile([P, BANK], U32, name="picked_words0%d" % s, align_bytes=64))
-        round_w8(0, 0)
-        round_w8(1, 1)
-        gather_scales(0, keep.tile([P, BANK], U8, name="picked_scales0", tag="word_window0", align_bytes=64))
+        picked_words0 = keep.tile([P, S], U32, name="picked_words0", align_bytes=64)
+        nc.vector.tensor_copy(picked_words0[:], word_window[0][:].bitcast(U32).indirect(offsets[:]))
+        picked_scales = keep.tile([P, S], U8, name="picked_scales", tag="word_window0", align_bytes=64)
+        nc.vector.tensor_copy(picked_scales[:], scale_window[:].indirect(offsets[:]))
+        round_w8(0)
+        round_w8(1)
         quantize_w8(0)
-        gather_scales(1, slot_tile(0, [P, BANK], U8, "picked_scales1"))
+        gather_ts(0, W8_BF16_SLOT[0])
         quantize_w8(1)
-        gather_scales(2, slot_tile(1, [P, BANK], U8, "picked_scales2"))
-        gather_ts(0, keep.tile([P, BANK], F32, name="picked_ts0"))
-        gather_words(1, 0, keep.tile([P, BANK], U32, name="picked_words10", tag="scale_window", align_bytes=64))
-        output_tile(0, 2)
-        output_tile(1, 3)
-        output_tile(2, 4)
-        gather_words(1, 1, slot_tile(2, [P, BANK], U32, "picked_words11"))
-        output_tile(3)
-        gather_ts(1, slot_tile(3, [P, BANK], F32, "picked_ts1"))
-        round_w8(2, 4)
-        output_tile(4, 5)
-        output_tile(5)
-        quantize_w8(2)
-        round_w8(3, 5)
-        output_tile(6)
-        output_tile(7)
-        quantize_w8(3)
-        for t in range(8, 24):
-            output_tile(t, {10: 6, 13: 7}.get(t))
-            if t == 12:
-                gather_words(1, 2, slot_tile(6, [P, BANK], U32, "picked_words12"))
-            if t == 14:
-                gather_ts(2, slot_tile(7, [P, BANK], F32, "picked_ts2"))
+        gather_ts(1, W8_BF16_SLOT[0] + 1)
+        gather_words1(0, W8_BF16_SLOT[1])
+        for t in range(len(TILES)):
+            if t == FIRST_TILE_OF_SLICE1:
+                gather_words1(1, W8_RAW_SLOT[1])
+            if t == WORDS2_GATHER_AT:
+                gather_words1(2, WORDS2_SLOT)
+            if t == TS2_GATHER_AT:
+                gather_ts(2, TS2_SLOT)
+            output_tile(t)

@@ -24,27 +24,33 @@ BANK = 512
 SLICES = S // BANK
 LIST_COLS = BANK // 16
 HALF = M // 2
+QUARTER = M // 4
 ROW_TILES = M // P
 LINE = 4
 QUADRANT = 32
 
 PLANE0 = 12
-SCALE_RUNS = ((0, 12, 16), (100, 28, 4), (12, 32, 0), (68, 32, 0), (44, 24, 4))
+SCALE_ROW0 = 96
+SCALE_RUNS = ((0, 4, 16), (12, 32, 0), (44, 4, 4), (64, 4, 24), (68, 32, 0), (108, 4, 12))
 
-TILES = [(s, 4 * h + c) for s, h in ((0, 0), (1, 0), (0, 1), (1, 1), (2, 0), (2, 1)) for c in range(4)]
-POOL_TILES = [(0, c) for c in range(0, ROW_TILES, 2)]
+TILES = [(s, c) for s in range(2) for c in range(4)] + [(2, 0), (0, 4), (2, 1), (2, 2), (2, 3), (1, 4), (2, 4), (0, 6), (0, 5), (1, 5), (2, 5), (1, 6), (2, 6), (0, 7), (1, 7), (2, 7)]
+POOL_TILES = [(0, 0), (0, 2), (0, 4), (0, 6)]
+POOL_BIAS = [(1, 2), (1, 3), (0, 5)]
+STORES = {(0, 1): (0, 1), (0, 3): (0, 1), (1, 0): (0, 2), (1, 2): (0, 2), (1, 1): (1, 2),
+          (2, 0): (2, 3), (2, 1): (2, 3), (2, 2): (2, 3), (2, 3): (1, 3), (2, 4): (0, 3), (2, 5): (0, 3), (2, 6): (0, 3),
+          (1, 7): (0, 2)}
 LAST_TILE_PIECES = 2
 
-SLOT_BYTES = 4 * BANK
-W8_BF16_SLOT = (0, 2)
-W8_RAW_SLOT = (4, 8)
-TS_COLS_OFFSET = W8_BF16_SLOT[1] * SLOT_BYTES - 64
-WORDS2_GATHER_AT, WORDS2_SLOT = 7, 13
-TS2_GATHER_AT, TS2_SLOT = 13, 12
-SCALED_SLOT = {WORDS2_GATHER_AT - 1: WORDS2_SLOT, TS2_GATHER_AT - 1: TS2_SLOT}
-FIRST_TILE_OF_SLICE1 = 4
-SCALED_BUFS = 10
-PLAIN_BUFS = len(POOL_TILES)
+KIB = 1024
+WORDS1_AT = 0
+SCALE_WINDOW_AT = 16 * KIB - 64
+W4_CODES_AT = 16 * KIB
+W8_LATE_AT = SCALE_WINDOW_AT + 4 * KIB - 64
+W8_BF16_AT = W8_LATE_AT + 8 * KIB
+TS_COLS_AT = W8_BF16_AT + 2 * KIB - 64
+HELD_AT = W8_BF16_AT + 4 * KIB
+SCALED_BUFS = 16
+PLAIN_BUFS = 4
 
 
 def tile_list_tabts_bias_kernel(
@@ -55,58 +61,65 @@ def tile_list_tabts_bias_kernel(
         keep = ctx.enter_context(tc.tile_pool(name="keep", bufs=1))
         ring = ctx.enter_context(tc.tile_pool(name="ring", bufs=1))
         shared = ctx.enter_context(tc.tile_pool(name="shared", bufs=1))
-        psum = ctx.enter_context(tc.psum_pool(name="psum", bufs=8))
+        psum = ctx.enter_context(tc.psum_pool(name="psum", bufs=1))
 
-        def slot_tile(slot, shape, dtype, name):
-            return shared.tile(shape, dtype, name=name, offset=slot * SLOT_BYTES, align_bytes=64)
+        def shared_tile(offset, shape, dtype, name):
+            return shared.tile(shape, dtype, name=name, offset=offset, align_bytes=64)
 
         offsets = keep.tile([P, S // 16], U16, name="offsets")
-        ts_cols = shared.tile([P, T // P], F32, name="ts_cols", offset=TS_COLS_OFFSET, align_bytes=64)
+        scale_window = shared_tile(SCALE_WINDOW_AT, [P, T // 4], I32, "scale_window")
+        ts_cols = shared_tile(TS_COLS_AT, [P, T // P], F32, "ts_cols")
         bias_rows = keep.tile([P, P], F32, name="bias_rows")
         ts_window = keep.tile([P, T], F32, name="ts_window", align_bytes=64)
-        scale_window = keep.tile([P, T], U8, name="scale_window", align_bytes=64)
-        word_window = [
-            keep.tile([P, T], I32, name="word_window%d" % a, tag="word_window%d" % a, align_bytes=64) for a in range(2)
-        ]
-        w8_raw = [slot_tile(W8_RAW_SLOT[h], [P, PACK, HALF], F32, "w8_raw%d" % h) for h in range(2)]
-        w8_codes = [keep.tile([P, HALF], U32, name="w8_codes%d" % h, align_bytes=64) for h in range(2)]
+        words0_window = keep.tile([P, T], I32, name="words0_window", tag="words0_window", align_bytes=64)
+        w8_early = keep.tile([P, PACK, HALF], F32, name="w8_early", align_bytes=64)
+        w8_codes = [keep.tile([P, QUARTER], U32, name="w8_codes%d" % q, align_bytes=64) for q in range(4)]
         w8_plane = keep.tile([P, M], U8, name="w8_plane", align_bytes=64)
-        w4_codes = keep.tile([P, 2 * M], U8, name="w4_codes", align_bytes=64)
         w4_plane = keep.tile([P, M // 4], I32, name="w4_plane", align_bytes=64)
+        picked_scales = keep.tile([P, S // 4], I32, name="picked_scales", align_bytes=64)
         bias = keep.tile([P, ROW_TILES], F32, name="bias")
         identity = keep.tile([P, P], F32, name="identity")
         results = [keep.tile([P, S], F32, name="result%d" % c) for c in range(ROW_TILES)]
         w8_bf16, picked_words1, picked_ts = {}, {}, {}
 
+        nc.vector.memset(scale_window[0:SCALE_ROW0, :], 0)
         make_identity(nc, identity[:])
-        nc.vector.memset(bias_rows[:], 0.0)
-        nc.vector.memset(w4_plane[:], 0)
+        nc.gpsimd.memset(picked_scales[:], 0)
+        nc.gpsimd.memset(bias_rows[:], 0.0)
+        nc.gpsimd.memset(w4_plane[:], 0)
 
-        def load_words(a):
-            nc.sync.dma_start(word_window[a][:], tab_words[a].rearrange("p t i -> p (t i)").bitcast(I32))
+        def table_words(a):
+            return tab_words[a].rearrange("p t i -> p (t i)").bitcast(I32)
 
-        nc.sync.dma_start(offsets[:], offs)
-        nc.sync.dma_start(ts_cols[:], ts[0].rearrange("(p c) -> p c", p=P))
-        load_words(0)
-        scale_rows = tab_scales.rearrange("a q t -> (a q) t").bitcast(I32)
-        for partition, count, row in SCALE_RUNS:
-            nc.sync.dma_start(
-                scale_window[:].bitcast(I32)[partition : partition + count, :], scale_rows[row : row + count, :]
-            )
-        nc.sync.dma_start(bias_rows[0:ROW_TILES, :], b.rearrange("(c x) -> c x", x=P))
         w8_by_partition = w8.rearrange("(p i) n -> p i n", i=PACK)
-        for h in range(2):
-            nc.sync.dma_start(w8_raw[h][:], w8_by_partition[:, :, h * HALF : (h + 1) * HALF])
-        nc.sync.dma_start(w4_codes[:].bitcast(I32), w4_words[0].bitcast(I32))
+        nc.sync.dma_start(offsets[:], offs)
+        nc.sync.dma_start(scale_window[SCALE_ROW0:P, :], tab_scales.rearrange("a q t -> (a q) t").bitcast(I32))
+        nc.sync.dma_start(ts_cols[:], ts[0].rearrange("(p c) -> p c", p=P))
+        nc.sync.dma_start(words0_window[:], table_words(0))
+        nc.sync.dma_start(w8_early[:], w8_by_partition[:, :, 0:HALF])
+        nc.gpsimd.dma_start(bias_rows[0:ROW_TILES, :], b.rearrange("(c x) -> c x", x=P))
         for q in range(P // QUADRANT):
-            nc.sync.dma_start(
+            nc.gpsimd.dma_start(
                 w4_plane[QUADRANT * q : QUADRANT * q + 4, :], w4_scales[0].bitcast(I32)[4 * q : 4 * q + 4, :]
             )
-        load_words(1)
+
+        picked_rows = keep.tile([P, S], U8, name="picked_rows", align_bytes=64)
+        nc.vector.tensor_copy(picked_rows[:], scale_window[:].bitcast(U8).indirect(offsets[:]))
+        for partition, count, row in SCALE_RUNS:
+            nc.sync.dma_start(
+                picked_scales[partition : partition + count, :],
+                picked_rows[:].bitcast(I32)[SCALE_ROW0 + row : SCALE_ROW0 + row + count, :],
+            )
+        words1_window = shared_tile(WORDS1_AT, [P, T], I32, "words1_window")
+        w4_codes = shared_tile(W4_CODES_AT, [P, 2 * M], U8, "w4_codes")
+        w8_late = shared_tile(W8_LATE_AT, [P, PACK, HALF], F32, "w8_late")
+        nc.sync.dma_start(words1_window[:], table_words(1))
+        nc.sync.dma_start(w4_codes[:].bitcast(I32), w4_words[0].bitcast(I32))
+        nc.sync.dma_start(w8_late[:], w8_by_partition[:, :, HALF:M])
 
         window_lines = ts_window[:].rearrange("q (p c) -> q p c", p=P)
         for g in range(T // BANK):
-            spread = psum.tile([P, BANK], F32, name="bank")
+            spread = psum.tile([P, BANK], F32, name="bank%d" % g)
             for i in range(LINE):
                 c = LINE * g + i
                 nc.tensor.transpose(
@@ -116,47 +129,52 @@ def tile_list_tabts_bias_kernel(
                 window_lines[:, :, LINE * g : LINE * (g + 1)], spread[:].rearrange("q (i p) -> q p i", i=LINE)
             )
 
-        bias_bank = psum.tile([P, BANK], F32, name="bank")
+        bias_bank = psum.tile([P, BANK], F32, name="bank7")
         nc.tensor.transpose(bias_bank[:, 0:P], bias_rows[:], identity[:])
         nc.scalar.copy(bias[:], bias_bank[:, 0:ROW_TILES])
 
         def list_slice(s):
             return offsets[:, s * LIST_COLS : (s + 1) * LIST_COLS]
 
-        def gather_words1(s, slot):
-            picked_words1[s] = slot_tile(slot, [P, BANK], U32, "picked_words1_%d" % s)
-            nc.vector.tensor_copy(picked_words1[s][:], word_window[1][:].bitcast(U32).indirect(list_slice(s)))
+        def gather_words1(s, tile):
+            picked_words1[s] = tile
+            nc.vector.tensor_copy(tile[:], words1_window[:].bitcast(U32).indirect(list_slice(s)))
 
-        def gather_ts(s, slot):
-            picked_ts[s] = slot_tile(slot, [P, BANK], F32, "picked_ts%d" % s)
-            nc.vector.tensor_copy(picked_ts[s][:], ts_window[:].indirect(list_slice(s)))
+        def gather_ts(s, tile):
+            picked_ts[s] = tile
+            nc.vector.tensor_copy(tile[:], ts_window[:].indirect(list_slice(s)))
 
-        def round_w8(h):
-            w8_bf16[h] = slot_tile(W8_BF16_SLOT[h], [P, HALF, PACK], BF16, "w8_bf16_%d" % h)
+        def round_w8(q):
+            raw = w8_early if q < 2 else w8_late
+            cols = slice((q % 2) * QUARTER, (q % 2 + 1) * QUARTER)
+            if q < 2:
+                w8_bf16[q] = shared_tile(W8_BF16_AT + 2 * KIB * q, [P, QUARTER, PACK], BF16, "w8_bf16_%d" % q)
+            else:
+                w8_bf16[q] = keep.tile([P, QUARTER, PACK], BF16, name="w8_bf16_%d" % q, align_bytes=64)
             nc.scalar.copy(
-                w8_bf16[h][:].rearrange("p (c u) i -> p c i u", u=LINE),
-                w8_raw[h][:].rearrange("p i (c u) -> p c i u", u=LINE),
+                w8_bf16[q][:].rearrange("p (c u) i -> p c i u", u=LINE),
+                raw[:, :, cols].rearrange("p i (c u) -> p c i u", u=LINE),
             )
 
-        def quantize_w8(h):
+        def quantize_w8(q):
             nc.vector.quantize_mx(
-                out=w8_codes[h][:].bitcast(FP8X4),
-                scales=w8_plane[:, h * HALF : (h + 1) * HALF],
-                in_=w8_bf16[h][:].rearrange("p n i -> p (n i)"),
+                out=w8_codes[q][:].bitcast(FP8X4),
+                scales=w8_plane[:, q * QUARTER : (q + 1) * QUARTER],
+                in_=w8_bf16[q][:].rearrange("p n i -> p (n i)"),
             )
 
         def output_tile(t):
             s, c = TILES[t]
             rows = slice(c * P, (c + 1) * P)
             entries = slice(s * BANK, (s + 1) * BANK)
-            h, first = divmod(c * P, HALF)
-            acc = psum.tile([P, BANK], F32, name="bank")
+            q, first = divmod(c * P, QUARTER)
+            acc = psum.tile([P, BANK], F32, name="bank%d" % (t % 8))
             nc.tensor.matmul_mx(
                 out=acc[:],
-                lhsT=w8_codes[h][:, first : first + P].bitcast(FP8X4),
+                lhsT=w8_codes[q][:, first : first + P].bitcast(FP8X4),
                 lhsT_scale=w8_plane[:, rows],
                 rhs=picked_words0[:, entries].bitcast(FP8X4),
-                rhs_scale=picked_scales[PLANE0:P, entries],
+                rhs_scale=picked_scales[:].bitcast(U8)[PLANE0:P, entries],
                 start=True,
                 stop=False,
             )
@@ -165,7 +183,7 @@ def tile_list_tabts_bias_kernel(
                 lhsT=w4_codes[:, 2 * c * P : 2 * (c + 1) * P].bitcast(FP4X4),
                 lhsT_scale=w4_plane[:].bitcast(U8)[:, rows],
                 rhs=picked_words1[s][:].bitcast(FP8X4),
-                rhs_scale=picked_scales[:, entries],
+                rhs_scale=picked_scales[:].bitcast(U8)[:, entries],
                 start=False,
                 stop=True,
             )
@@ -177,36 +195,43 @@ def tile_list_tabts_bias_kernel(
                 nc.gpsimd.tensor_tensor(scaled[:], plain[:], picked_ts[s][:], MULT)
                 nc.gpsimd.tensor_scalar(results[c][:, entries], scaled[:], 1.0, bias_column, MULT, ADD)
                 return
-            if t in SCALED_SLOT:
-                scaled = slot_tile(SCALED_SLOT[t], [P, BANK], F32, "scaled%d" % t)
+            if (s, c) == (1, 0):
+                scaled = shared_tile(HELD_AT, [P, BANK], F32, "scaled_held")
             else:
                 scaled = ring.tile([P, BANK], F32, name="scaled", bufs=SCALED_BUFS)
-            width = BANK // (LAST_TILE_PIECES if t == len(TILES) - 1 else 1)
+            last = t == len(TILES) - 1
+            width = BANK // (LAST_TILE_PIECES if last else 1)
             for start in range(0, BANK, width):
                 part = slice(start, start + width)
                 cols = slice(s * BANK + start, s * BANK + start + width)
                 nc.vector.tensor_tensor(scaled[:, part], acc[:, part], picked_ts[s][:, part], MULT)
-                nc.scalar.activation(results[c][:, cols], scaled[:, part], IDENTITY, bias=bias_column)
-                if (s - 1, c) in POOL_TILES:
-                    cols = slice(cols.start - BANK, cols.stop)
-                nc.sync.dma_start(out[rows, cols], results[c][:, cols])
+                if (s, c) in POOL_BIAS:
+                    nc.gpsimd.tensor_scalar(results[c][:, cols], scaled[:, part], 1.0, bias_column, MULT, ADD)
+                else:
+                    nc.scalar.activation(results[c][:, cols], scaled[:, part], IDENTITY, bias=bias_column)
+                if last:
+                    nc.sync.dma_start(out[rows, cols], results[c][:, cols])
+            if (s, c) in STORES:
+                lo, hi = STORES[(s, c)]
+                nc.sync.dma_start(out[rows, lo * BANK : hi * BANK], results[c][:, lo * BANK : hi * BANK])
 
         picked_words0 = keep.tile([P, S], U32, name="picked_words0", align_bytes=64)
-        nc.vector.tensor_copy(picked_words0[:], word_window[0][:].bitcast(U32).indirect(offsets[:]))
-        picked_scales = keep.tile([P, S], U8, name="picked_scales", tag="word_window0", align_bytes=64)
-        nc.vector.tensor_copy(picked_scales[:], scale_window[:].indirect(offsets[:]))
+        nc.vector.tensor_copy(picked_words0[:], words0_window[:].bitcast(U32).indirect(offsets[:]))
         round_w8(0)
         round_w8(1)
         quantize_w8(0)
-        gather_ts(0, W8_BF16_SLOT[0])
+        gather_ts(0, shared_tile(W8_BF16_AT, [P, BANK], F32, "picked_ts0"))
         quantize_w8(1)
-        gather_ts(1, W8_BF16_SLOT[0] + 1)
-        gather_words1(0, W8_BF16_SLOT[1])
+        gather_ts(1, shared_tile(W8_BF16_AT + 2 * KIB, [P, BANK], F32, "picked_ts1"))
+        for s in range(2):
+            gather_words1(s, keep.tile([P, BANK], U32, name="picked_words1_%d" % s, align_bytes=64))
         for t in range(len(TILES)):
-            if t == FIRST_TILE_OF_SLICE1:
-                gather_words1(1, W8_RAW_SLOT[1])
-            if t == WORDS2_GATHER_AT:
-                gather_words1(2, WORDS2_SLOT)
-            if t == TS2_GATHER_AT:
-                gather_ts(2, TS2_SLOT)
+            if t == 8:
+                round_w8(2)
+                round_w8(3)
+                gather_words1(2, shared_tile(HELD_AT, [P, BANK], U32, "picked_words1_2"))
+                gather_ts(2, shared_tile(WORDS1_AT, [P, BANK], F32, "picked_ts2"))
+                quantize_w8(2)
+            if t == 12:
+                quantize_w8(3)
             output_tile(t)

@@ -31,14 +31,12 @@ QUADRANT = 32
 
 PLANE0 = 12
 SCALE_ROW0 = 96
-SCALE_RUNS = ((0, 4, 16), (12, 32, 0), (44, 4, 4), (64, 4, 24), (68, 32, 0), (108, 4, 12))
+SCALE_RUNS = ((0, 4, 16), (4, 32, -8), (36, 32, -4), (68, 32, 0), (108, 4, 12))
 
-TILES = [(s, c) for s in range(2) for c in range(4)] + [(2, 0), (0, 4), (2, 1), (2, 2), (2, 3), (1, 4), (2, 4), (0, 6), (0, 5), (1, 5), (2, 5), (1, 6), (2, 6), (0, 7), (1, 7), (2, 7)]
-POOL_TILES = [(0, 0), (0, 2), (0, 4), (0, 6)]
-POOL_BIAS = [(1, 2), (1, 3), (0, 5)]
-STORES = {(0, 1): (0, 1), (0, 3): (0, 1), (1, 0): (0, 2), (1, 2): (0, 2), (1, 1): (1, 2),
-          (2, 0): (2, 3), (2, 1): (2, 3), (2, 2): (2, 3), (2, 3): (1, 3), (2, 4): (0, 3), (2, 5): (0, 3), (2, 6): (0, 3),
-          (1, 7): (0, 2)}
+TILES = [(0, 0), (0, 1), (0, 2), (0, 3), (1, 0), (1, 1), (1, 2), (0, 4), (1, 3), (1, 4), (0, 5), (0, 6), (1, 5),
+         (2, 0), (2, 1), (0, 7), (2, 2), (2, 3), (1, 6), (2, 4), (2, 5), (2, 6), (1, 7), (2, 7)]
+POOL_TILES = [(0, 0), (0, 2), (0, 4), (0, 6), (0, 7)]
+POOL_BIAS = [(2, 6)]
 LAST_TILE_PIECES = 2
 
 KIB = 1024
@@ -46,11 +44,13 @@ WORDS1_AT = 0
 SCALE_WINDOW_AT = 16 * KIB - 64
 W4_CODES_AT = 16 * KIB
 W8_LATE_AT = SCALE_WINDOW_AT + 4 * KIB - 64
-W8_BF16_AT = W8_LATE_AT + 8 * KIB
+W8_LAST_AT = W8_LATE_AT + 4 * KIB
+W8_EARLY_AT = W8_LAST_AT + 4 * KIB
+W8_BF16_AT = W8_EARLY_AT + 8 * KIB
 TS_COLS_AT = W8_BF16_AT + 2 * KIB - 64
 HELD_AT = W8_BF16_AT + 4 * KIB
 SCALED_BUFS = 16
-PLAIN_BUFS = 4
+PLAIN_BUFS = 1
 
 
 def tile_list_tabts_bias_kernel(
@@ -72,12 +72,11 @@ def tile_list_tabts_bias_kernel(
         bias_rows = keep.tile([P, P], F32, name="bias_rows")
         ts_window = keep.tile([P, T], F32, name="ts_window", align_bytes=64)
         words0_window = keep.tile([P, T], I32, name="words0_window", tag="words0_window", align_bytes=64)
-        w8_early = keep.tile([P, PACK, HALF], F32, name="w8_early", align_bytes=64)
+        w8_early = [shared_tile(W8_EARLY_AT + 4 * KIB * q, [P, PACK, QUARTER], F32, "w8_early%d" % q) for q in range(2)]
         w8_codes = [keep.tile([P, QUARTER], U32, name="w8_codes%d" % q, align_bytes=64) for q in range(4)]
         w8_plane = keep.tile([P, M], U8, name="w8_plane", align_bytes=64)
         w4_plane = keep.tile([P, M // 4], I32, name="w4_plane", align_bytes=64)
         picked_scales = keep.tile([P, S // 4], I32, name="picked_scales", align_bytes=64)
-        bias = keep.tile([P, ROW_TILES], F32, name="bias")
         identity = keep.tile([P, P], F32, name="identity")
         results = [keep.tile([P, S], F32, name="result%d" % c) for c in range(ROW_TILES)]
         w8_bf16, picked_words1, picked_ts = {}, {}, {}
@@ -96,14 +95,15 @@ def tile_list_tabts_bias_kernel(
         nc.sync.dma_start(scale_window[SCALE_ROW0:P, :], tab_scales.rearrange("a q t -> (a q) t").bitcast(I32))
         nc.sync.dma_start(ts_cols[:], ts[0].rearrange("(p c) -> p c", p=P))
         nc.sync.dma_start(words0_window[:], table_words(0))
-        nc.sync.dma_start(w8_early[:], w8_by_partition[:, :, 0:HALF])
+        for q in range(2):
+            nc.sync.dma_start(w8_early[q][:], w8_by_partition[:, :, q * QUARTER : (q + 1) * QUARTER])
         nc.gpsimd.dma_start(bias_rows[0:ROW_TILES, :], b.rearrange("(c x) -> c x", x=P))
         for q in range(P // QUADRANT):
             nc.gpsimd.dma_start(
                 w4_plane[QUADRANT * q : QUADRANT * q + 4, :], w4_scales[0].bitcast(I32)[4 * q : 4 * q + 4, :]
             )
 
-        picked_rows = keep.tile([P, S], U8, name="picked_rows", align_bytes=64)
+        picked_rows = shared_tile(W8_LAST_AT, [P, S], U8, "picked_rows")
         nc.vector.tensor_copy(picked_rows[:], scale_window[:].bitcast(U8).indirect(offsets[:]))
         for partition, count, row in SCALE_RUNS:
             nc.sync.dma_start(
@@ -112,10 +112,12 @@ def tile_list_tabts_bias_kernel(
             )
         words1_window = shared_tile(WORDS1_AT, [P, T], I32, "words1_window")
         w4_codes = shared_tile(W4_CODES_AT, [P, 2 * M], U8, "w4_codes")
-        w8_late = shared_tile(W8_LATE_AT, [P, PACK, HALF], F32, "w8_late")
+        w8_late = shared_tile(W8_LATE_AT, [P, PACK, QUARTER], F32, "w8_late")
+        w8_last = shared_tile(W8_LAST_AT, [P, PACK, QUARTER], F32, "w8_last")
         nc.sync.dma_start(words1_window[:], table_words(1))
+        nc.sync.dma_start(w8_late[:], w8_by_partition[:, :, HALF : HALF + QUARTER])
         nc.sync.dma_start(w4_codes[:].bitcast(I32), w4_words[0].bitcast(I32))
-        nc.sync.dma_start(w8_late[:], w8_by_partition[:, :, HALF:M])
+        nc.sync.dma_start(w8_last[:], w8_by_partition[:, :, HALF + QUARTER : M])
 
         window_lines = ts_window[:].rearrange("q (p c) -> q p c", p=P)
         for g in range(T // BANK):
@@ -131,7 +133,6 @@ def tile_list_tabts_bias_kernel(
 
         bias_bank = psum.tile([P, BANK], F32, name="bank7")
         nc.tensor.transpose(bias_bank[:, 0:P], bias_rows[:], identity[:])
-        nc.scalar.copy(bias[:], bias_bank[:, 0:ROW_TILES])
 
         def list_slice(s):
             return offsets[:, s * LIST_COLS : (s + 1) * LIST_COLS]
@@ -140,20 +141,22 @@ def tile_list_tabts_bias_kernel(
             picked_words1[s] = tile
             nc.vector.tensor_copy(tile[:], words1_window[:].bitcast(U32).indirect(list_slice(s)))
 
-        def gather_ts(s, tile):
-            picked_ts[s] = tile
-            nc.vector.tensor_copy(tile[:], ts_window[:].indirect(list_slice(s)))
+        def gather_ts(first, count, tile):
+            for s in range(count):
+                picked_ts[first + s] = tile[:, s * BANK : (s + 1) * BANK]
+            nc.vector.tensor_copy(
+                tile[:], ts_window[:].indirect(offsets[:, first * LIST_COLS : (first + count) * LIST_COLS])
+            )
 
         def round_w8(q):
-            raw = w8_early if q < 2 else w8_late
-            cols = slice((q % 2) * QUARTER, (q % 2 + 1) * QUARTER)
+            raw = (w8_early[0][:], w8_early[1][:], w8_late[:], w8_last[:])[q]
             if q < 2:
                 w8_bf16[q] = shared_tile(W8_BF16_AT + 2 * KIB * q, [P, QUARTER, PACK], BF16, "w8_bf16_%d" % q)
             else:
                 w8_bf16[q] = keep.tile([P, QUARTER, PACK], BF16, name="w8_bf16_%d" % q, align_bytes=64)
             nc.scalar.copy(
                 w8_bf16[q][:].rearrange("p (c u) i -> p c i u", u=LINE),
-                raw[:, :, cols].rearrange("p i (c u) -> p c i u", u=LINE),
+                raw.rearrange("p i (c u) -> p c i u", u=LINE),
             )
 
         def quantize_w8(q):
@@ -190,13 +193,20 @@ def tile_list_tabts_bias_kernel(
             bias_column = bias[:, c : c + 1]
             if (s, c) in POOL_TILES:
                 scaled = ring.tile([P, BANK], F32, name="scaled_pool")
-                plain = ring.tile([P, BANK], F32, name="plain", bufs=PLAIN_BUFS)
+                if t < 4:
+                    plain = ring.tile([P, BANK], F32, name="plain_first")
+                else:
+                    plain = ring.tile([P, BANK], F32, name="plain", bufs=4)
                 nc.scalar.copy(plain[:], acc[:])
-                nc.gpsimd.tensor_tensor(scaled[:], plain[:], picked_ts[s][:], MULT)
+                nc.gpsimd.tensor_tensor(scaled[:], plain[:], picked_ts[s], MULT)
                 nc.gpsimd.tensor_scalar(results[c][:, entries], scaled[:], 1.0, bias_column, MULT, ADD)
+                if s > 0:
+                    nc.sync.dma_start(out[rows, entries], results[c][:, entries])
                 return
             if (s, c) == (1, 0):
                 scaled = shared_tile(HELD_AT, [P, BANK], F32, "scaled_held")
+            elif (s, c) == (1, 4):
+                scaled = shared_tile(HELD_AT + 2 * KIB, [P, BANK], F32, "scaled_held2")
             else:
                 scaled = ring.tile([P, BANK], F32, name="scaled", bufs=SCALED_BUFS)
             last = t == len(TILES) - 1
@@ -211,27 +221,32 @@ def tile_list_tabts_bias_kernel(
                     nc.scalar.activation(results[c][:, cols], scaled[:, part], IDENTITY, bias=bias_column)
                 if last:
                     nc.sync.dma_start(out[rows, cols], results[c][:, cols])
-            if (s, c) in STORES:
-                lo, hi = STORES[(s, c)]
-                nc.sync.dma_start(out[rows, lo * BANK : hi * BANK], results[c][:, lo * BANK : hi * BANK])
+            paired = c % 2 == 0 or c >= 4
+            if s == 1 and paired:
+                nc.sync.dma_start(out[rows, 0 : 2 * BANK], results[c][:, 0 : 2 * BANK])
+            elif not last and (s == 2 or not paired):
+                nc.sync.dma_start(out[rows, entries], results[c][:, entries])
 
         picked_words0 = keep.tile([P, S], U32, name="picked_words0", align_bytes=64)
         nc.vector.tensor_copy(picked_words0[:], words0_window[:].bitcast(U32).indirect(offsets[:]))
         round_w8(0)
         round_w8(1)
+        bias = shared_tile(W8_EARLY_AT + 7 * KIB, [P, ROW_TILES], F32, "bias")
+        nc.scalar.copy(bias[:], bias_bank[:, 0:ROW_TILES])
         quantize_w8(0)
-        gather_ts(0, shared_tile(W8_BF16_AT, [P, BANK], F32, "picked_ts0"))
         quantize_w8(1)
-        gather_ts(1, shared_tile(W8_BF16_AT + 2 * KIB, [P, BANK], F32, "picked_ts1"))
+        gather_ts(0, 2, shared_tile(W8_EARLY_AT + 2 * KIB, [P, 2 * BANK], F32, "picked_ts01"))
         for s in range(2):
             gather_words1(s, keep.tile([P, BANK], U32, name="picked_words1_%d" % s, align_bytes=64))
+        round_w8(2)
         for t in range(len(TILES)):
-            if t == 8:
-                round_w8(2)
-                round_w8(3)
-                gather_words1(2, shared_tile(HELD_AT, [P, BANK], U32, "picked_words1_2"))
-                gather_ts(2, shared_tile(WORDS1_AT, [P, BANK], F32, "picked_ts2"))
+            if t == 4:
                 quantize_w8(2)
-            if t == 12:
+            if t == 5:
+                round_w8(3)
+            if t == 9:
+                gather_words1(2, shared_tile(HELD_AT, [P, BANK], U32, "picked_words1_2"))
                 quantize_w8(3)
+            if t == 13:
+                gather_ts(2, 1, shared_tile(HELD_AT + 2 * KIB, [P, BANK], F32, "picked_ts2"))
             output_tile(t)

@@ -33,10 +33,12 @@ PLANE0 = 12
 SCALE_ROW0 = 96
 SCALE_RUNS = ((0, 4, 16), (4, 32, -8), (36, 32, -4), (68, 32, 0), (108, 4, 12))
 
-TILES = [(0, 0), (0, 1), (0, 2), (0, 3), (1, 0), (1, 1), (1, 2), (0, 4), (1, 3), (1, 4), (0, 5), (0, 6), (1, 5),
-         (2, 0), (2, 1), (0, 7), (2, 2), (2, 3), (1, 6), (2, 4), (2, 5), (2, 6), (1, 7), (2, 7)]
-POOL_TILES = [(0, 0), (0, 2), (0, 4), (0, 6), (0, 7)]
-POOL_BIAS = [(2, 6)]
+TILES = [(s, c) for s in range(2) for c in range(4)] + [(2, 0), (0, 4), (2, 1), (2, 2), (2, 3), (1, 4), (0, 6),
+         (2, 4), (0, 5), (1, 5), (2, 5), (1, 6), (2, 6), (0, 7), (1, 7), (2, 7)]
+POOL_TILES = [(0, 0), (0, 2), (0, 4), (0, 6)]
+POOL_BIAS = [(1, 3), (2, 0), (0, 7)]
+STORE_FROM = {(0, 1): 0, (0, 3): 0, (1, 0): 0, (1, 1): 1, (1, 2): 0, (1, 3): 1, (2, 0): 2, (2, 1): 2, (2, 2): 2, (2, 3): 2,
+              (1, 4): 0, (2, 4): 2, (2, 5): 0, (2, 6): 0, (1, 7): 0}
 LAST_TILE_PIECES = 2
 
 KIB = 1024
@@ -72,7 +74,7 @@ def tile_list_tabts_bias_kernel(
         bias_rows = keep.tile([P, P], F32, name="bias_rows")
         ts_window = keep.tile([P, T], F32, name="ts_window", align_bytes=64)
         words0_window = keep.tile([P, T], I32, name="words0_window", tag="words0_window", align_bytes=64)
-        w8_early = [shared_tile(W8_EARLY_AT + 4 * KIB * q, [P, PACK, QUARTER], F32, "w8_early%d" % q) for q in range(2)]
+        w8_early = shared_tile(W8_EARLY_AT, [P, PACK, HALF], F32, "w8_early")
         w8_codes = [keep.tile([P, QUARTER], U32, name="w8_codes%d" % q, align_bytes=64) for q in range(4)]
         w8_plane = keep.tile([P, M], U8, name="w8_plane", align_bytes=64)
         w4_plane = keep.tile([P, M // 4], I32, name="w4_plane", align_bytes=64)
@@ -95,8 +97,7 @@ def tile_list_tabts_bias_kernel(
         nc.sync.dma_start(scale_window[SCALE_ROW0:P, :], tab_scales.rearrange("a q t -> (a q) t").bitcast(I32))
         nc.sync.dma_start(ts_cols[:], ts[0].rearrange("(p c) -> p c", p=P))
         nc.sync.dma_start(words0_window[:], table_words(0))
-        for q in range(2):
-            nc.sync.dma_start(w8_early[q][:], w8_by_partition[:, :, q * QUARTER : (q + 1) * QUARTER])
+        nc.sync.dma_start(w8_early[:], w8_by_partition[:, :, 0:HALF])
         nc.gpsimd.dma_start(bias_rows[0:ROW_TILES, :], b.rearrange("(c x) -> c x", x=P))
         for q in range(P // QUADRANT):
             nc.gpsimd.dma_start(
@@ -115,8 +116,8 @@ def tile_list_tabts_bias_kernel(
         w8_late = shared_tile(W8_LATE_AT, [P, PACK, QUARTER], F32, "w8_late")
         w8_last = shared_tile(W8_LAST_AT, [P, PACK, QUARTER], F32, "w8_last")
         nc.sync.dma_start(words1_window[:], table_words(1))
-        nc.sync.dma_start(w8_late[:], w8_by_partition[:, :, HALF : HALF + QUARTER])
         nc.sync.dma_start(w4_codes[:].bitcast(I32), w4_words[0].bitcast(I32))
+        nc.sync.dma_start(w8_late[:], w8_by_partition[:, :, HALF : HALF + QUARTER])
         nc.sync.dma_start(w8_last[:], w8_by_partition[:, :, HALF + QUARTER : M])
 
         window_lines = ts_window[:].rearrange("q (p c) -> q p c", p=P)
@@ -149,11 +150,11 @@ def tile_list_tabts_bias_kernel(
             )
 
         def round_w8(q):
-            raw = (w8_early[0][:], w8_early[1][:], w8_late[:], w8_last[:])[q]
+            raw = (w8_early[:, :, 0:QUARTER], w8_early[:, :, QUARTER:HALF], w8_late[:], w8_last[:])[q]
             if q < 2:
                 w8_bf16[q] = shared_tile(W8_BF16_AT + 2 * KIB * q, [P, QUARTER, PACK], BF16, "w8_bf16_%d" % q)
             else:
-                w8_bf16[q] = keep.tile([P, QUARTER, PACK], BF16, name="w8_bf16_%d" % q, align_bytes=64)
+                w8_bf16[q] = shared_tile(HELD_AT + 2 * KIB * (q - 1), [P, QUARTER, PACK], BF16, "w8_bf16_%d" % q)
             nc.scalar.copy(
                 w8_bf16[q][:].rearrange("p (c u) i -> p c i u", u=LINE),
                 raw.rearrange("p i (c u) -> p c i u", u=LINE),
@@ -194,19 +195,15 @@ def tile_list_tabts_bias_kernel(
             if (s, c) in POOL_TILES:
                 scaled = ring.tile([P, BANK], F32, name="scaled_pool")
                 if t < 4:
-                    plain = ring.tile([P, BANK], F32, name="plain_first")
+                    plain = shared_tile(HELD_AT + (2 + t) * KIB, [P, BANK], F32, "plain_first%d" % t)
                 else:
-                    plain = ring.tile([P, BANK], F32, name="plain", bufs=4)
+                    plain = ring.tile([P, BANK], F32, name="plain", bufs=2)
                 nc.scalar.copy(plain[:], acc[:])
                 nc.gpsimd.tensor_tensor(scaled[:], plain[:], picked_ts[s], MULT)
                 nc.gpsimd.tensor_scalar(results[c][:, entries], scaled[:], 1.0, bias_column, MULT, ADD)
-                if s > 0:
-                    nc.sync.dma_start(out[rows, entries], results[c][:, entries])
                 return
-            if (s, c) == (1, 0):
+            if (s, c) == (0, 1):
                 scaled = shared_tile(HELD_AT, [P, BANK], F32, "scaled_held")
-            elif (s, c) == (1, 4):
-                scaled = shared_tile(HELD_AT + 2 * KIB, [P, BANK], F32, "scaled_held2")
             else:
                 scaled = ring.tile([P, BANK], F32, name="scaled", bufs=SCALED_BUFS)
             last = t == len(TILES) - 1
@@ -221,11 +218,9 @@ def tile_list_tabts_bias_kernel(
                     nc.scalar.activation(results[c][:, cols], scaled[:, part], IDENTITY, bias=bias_column)
                 if last:
                     nc.sync.dma_start(out[rows, cols], results[c][:, cols])
-            paired = c % 2 == 0 or c >= 4
-            if s == 1 and paired:
-                nc.sync.dma_start(out[rows, 0 : 2 * BANK], results[c][:, 0 : 2 * BANK])
-            elif not last and (s == 2 or not paired):
-                nc.sync.dma_start(out[rows, entries], results[c][:, entries])
+            if (s, c) in STORE_FROM:
+                cols = slice(STORE_FROM[(s, c)] * BANK, (s + 1) * BANK)
+                nc.sync.dma_start(out[rows, cols], results[c][:, cols])
 
         picked_words0 = keep.tile([P, S], U32, name="picked_words0", align_bytes=64)
         nc.vector.tensor_copy(picked_words0[:], words0_window[:].bitcast(U32).indirect(offsets[:]))
@@ -233,20 +228,19 @@ def tile_list_tabts_bias_kernel(
         round_w8(1)
         bias = shared_tile(W8_EARLY_AT + 7 * KIB, [P, ROW_TILES], F32, "bias")
         nc.scalar.copy(bias[:], bias_bank[:, 0:ROW_TILES])
+        gather_ts(0, 1, keep.tile([P, BANK], F32, name="picked_ts0", align_bytes=64))
         quantize_w8(0)
         quantize_w8(1)
-        gather_ts(0, 2, shared_tile(W8_EARLY_AT + 2 * KIB, [P, 2 * BANK], F32, "picked_ts01"))
+        gather_ts(1, 2, shared_tile(W8_EARLY_AT, [P, 2 * BANK], F32, "picked_ts12"))
         for s in range(2):
             gather_words1(s, keep.tile([P, BANK], U32, name="picked_words1_%d" % s, align_bytes=64))
-        round_w8(2)
         for t in range(len(TILES)):
-            if t == 4:
-                quantize_w8(2)
-            if t == 5:
-                round_w8(3)
-            if t == 9:
+            if t == 6:
+                round_w8(2)
                 gather_words1(2, shared_tile(HELD_AT, [P, BANK], U32, "picked_words1_2"))
-                quantize_w8(3)
+            if t == 8:
+                round_w8(3)
+                quantize_w8(2)
             if t == 13:
-                gather_ts(2, 1, shared_tile(HELD_AT + 2 * KIB, [P, BANK], F32, "picked_ts2"))
+                quantize_w8(3)
             output_tile(t)

@@ -21,38 +21,60 @@ IDENTITY = mybir.ActivationFunctionType.Identity
 P = 128
 PACK = 4
 BANK = 512
+BANKS = 8
 SLICES = S // BANK
 LIST_COLS = BANK // 16
 HALF = M // 2
 QUARTER = M // 4
 ROW_TILES = M // P
+EARLY_ROWS = ROW_TILES // 2
 LINE = 4
 QUADRANT = 32
 
+SCALE_ROW0 = P - QUADRANT
 PLANE0 = 12
-SCALE_ROW0 = 96
 SCALE_RUNS = ((0, 4, 16), (4, 32, -8), (36, 32, -4), (68, 32, 0), (108, 4, 12))
 
-TILES = [(s, c) for s in range(2) for c in range(4)] + [(2, 0), (0, 4), (2, 1), (2, 2), (2, 3), (1, 4), (0, 6),
-         (2, 4), (0, 5), (1, 5), (2, 5), (1, 6), (2, 6), (0, 7), (1, 7), (2, 7)]
-POOL_TILES = [(0, 0), (0, 2), (0, 4), (0, 6)]
-POOL_BIAS = [(1, 3), (2, 0), (0, 7)]
-STORE_FROM = {(0, 1): 0, (0, 3): 0, (1, 0): 0, (1, 1): 1, (1, 2): 0, (1, 3): 1, (2, 0): 2, (2, 1): 2, (2, 2): 2, (2, 3): 2,
-              (1, 4): 0, (2, 4): 2, (2, 5): 0, (2, 6): 0, (1, 7): 0}
-LAST_TILE_PIECES = 2
+POOL_TILES = [(0, c) for c in range(0, ROW_TILES, 2)]
+POOL_LEAD = 5
+POOL_BIASES = [(1, EARLY_ROWS - 1), (2, 0), (2, 1)]
+LAST_GATHER_AT = 6
+SCALED_BUFS = 16
+PLAIN_BUFS = 2
 
 KIB = 1024
+OVERLAP = 64
+TILE_BYTES = 4 * BANK
 WORDS1_AT = 0
-SCALE_WINDOW_AT = 16 * KIB - 64
+SCALE_WINDOW_AT = 16 * KIB - OVERLAP
 W4_CODES_AT = 16 * KIB
-W8_LATE_AT = SCALE_WINDOW_AT + 4 * KIB - 64
-W8_LAST_AT = W8_LATE_AT + 4 * KIB
-W8_EARLY_AT = W8_LAST_AT + 4 * KIB
-W8_BF16_AT = W8_EARLY_AT + 8 * KIB
-TS_COLS_AT = W8_BF16_AT + 2 * KIB - 64
-HELD_AT = W8_BF16_AT + 4 * KIB
-SCALED_BUFS = 16
-PLAIN_BUFS = 1
+PICKED_TS0_AT = 20 * KIB
+W8_LATE_AT = 22 * KIB
+PICKED_ROWS_AT = W8_LATE_AT - S // 2
+W8_EARLY_AT = 30 * KIB
+BIAS_AT = W8_EARLY_AT + 2 * TILE_BYTES
+EARLY_BF16_AT = 38 * KIB
+TS_COLS_AT = EARLY_BF16_AT + TILE_BYTES - OVERLAP
+FIRST_SCALED_AT = 42 * KIB
+LATE_BF16_AT = 44 * KIB
+
+
+def tile_order():
+    order = [(s, c) for s in range(SLICES) for c in range(EARLY_ROWS)]
+    for even in range(EARLY_ROWS, ROW_TILES, 2):
+        odd = even + 1
+        order = order + [(0, odd), (1, even), (1, odd), (2, odd), (2, even)]
+        at = order.index((1, even)) - POOL_LEAD
+        order = order[:at] + [(0, even)] + order[at:]
+    return order
+
+
+def first_stored_slice(s, c):
+    if s == 1 and (0, c) in POOL_TILES:
+        return 0
+    if c >= EARLY_ROWS and (0, c) not in POOL_TILES and s > 0:
+        return 1 if s == 2 else None
+    return s
 
 
 def tile_list_tabts_bias_kernel(
@@ -68,26 +90,36 @@ def tile_list_tabts_bias_kernel(
         def shared_tile(offset, shape, dtype, name):
             return shared.tile(shape, dtype, name=name, offset=offset, align_bytes=64)
 
+        def bank(i):
+            return psum.tile([P, BANK], F32, name="bank%d" % (i % BANKS))
+
         offsets = keep.tile([P, S // 16], U16, name="offsets")
         scale_window = shared_tile(SCALE_WINDOW_AT, [P, T // 4], I32, "scale_window")
         ts_cols = shared_tile(TS_COLS_AT, [P, T // P], F32, "ts_cols")
+        w8_early = shared_tile(W8_EARLY_AT, [P, PACK, HALF], F32, "w8_early")
         bias_rows = keep.tile([P, P], F32, name="bias_rows")
         ts_window = keep.tile([P, T], F32, name="ts_window", align_bytes=64)
-        words0_window = keep.tile([P, T], I32, name="words0_window", tag="words0_window", align_bytes=64)
-        w8_early = shared_tile(W8_EARLY_AT, [P, PACK, HALF], F32, "w8_early")
+        words0_window = keep.tile([P, T], I32, name="words0_window", align_bytes=64)
         w8_codes = [keep.tile([P, QUARTER], U32, name="w8_codes%d" % q, align_bytes=64) for q in range(4)]
         w8_plane = keep.tile([P, M], U8, name="w8_plane", align_bytes=64)
         w4_plane = keep.tile([P, M // 4], I32, name="w4_plane", align_bytes=64)
-        picked_scales = keep.tile([P, S // 4], I32, name="picked_scales", align_bytes=64)
+        table_planes = keep.tile([P, S // 4], I32, name="table_planes", align_bytes=64)
         identity = keep.tile([P, P], F32, name="identity")
         results = [keep.tile([P, S], F32, name="result%d" % c) for c in range(ROW_TILES)]
         w8_bf16, picked_words1, picked_ts = {}, {}, {}
+        order = tile_order()
 
+        nc.vector.memset(bias_rows[:], 0.0)
+        nc.vector.memset(w4_plane[:], 0)
         nc.vector.memset(scale_window[0:SCALE_ROW0, :], 0)
+        nc.vector.memset(table_planes[:], 0)
         make_identity(nc, identity[:])
-        nc.gpsimd.memset(picked_scales[:], 0)
-        nc.gpsimd.memset(bias_rows[:], 0.0)
-        nc.gpsimd.memset(w4_plane[:], 0)
+
+        nc.gpsimd.dma_start(bias_rows[0:ROW_TILES, :], b.rearrange("(c x) -> c x", x=P))
+        for q in range(P // QUADRANT):
+            nc.gpsimd.dma_start(
+                w4_plane[QUADRANT * q : QUADRANT * q + 4, :], w4_scales[0].bitcast(I32)[4 * q : 4 * q + 4, :]
+            )
 
         def table_words(a):
             return tab_words[a].rearrange("p t i -> p (t i)").bitcast(I32)
@@ -98,31 +130,25 @@ def tile_list_tabts_bias_kernel(
         nc.sync.dma_start(ts_cols[:], ts[0].rearrange("(p c) -> p c", p=P))
         nc.sync.dma_start(words0_window[:], table_words(0))
         nc.sync.dma_start(w8_early[:], w8_by_partition[:, :, 0:HALF])
-        nc.gpsimd.dma_start(bias_rows[0:ROW_TILES, :], b.rearrange("(c x) -> c x", x=P))
-        for q in range(P // QUADRANT):
-            nc.gpsimd.dma_start(
-                w4_plane[QUADRANT * q : QUADRANT * q + 4, :], w4_scales[0].bitcast(I32)[4 * q : 4 * q + 4, :]
-            )
 
-        picked_rows = shared_tile(W8_LAST_AT, [P, S], U8, "picked_rows")
+        picked_rows = shared_tile(PICKED_ROWS_AT, [P, S], U8, "picked_rows")
         nc.vector.tensor_copy(picked_rows[:], scale_window[:].bitcast(U8).indirect(offsets[:]))
         for partition, count, row in SCALE_RUNS:
             nc.sync.dma_start(
-                picked_scales[partition : partition + count, :],
+                table_planes[partition : partition + count, :],
                 picked_rows[:].bitcast(I32)[SCALE_ROW0 + row : SCALE_ROW0 + row + count, :],
             )
+
         words1_window = shared_tile(WORDS1_AT, [P, T], I32, "words1_window")
         w4_codes = shared_tile(W4_CODES_AT, [P, 2 * M], U8, "w4_codes")
-        w8_late = shared_tile(W8_LATE_AT, [P, PACK, QUARTER], F32, "w8_late")
-        w8_last = shared_tile(W8_LAST_AT, [P, PACK, QUARTER], F32, "w8_last")
+        w8_late = shared_tile(W8_LATE_AT, [P, PACK, HALF], F32, "w8_late")
         nc.sync.dma_start(words1_window[:], table_words(1))
         nc.sync.dma_start(w4_codes[:].bitcast(I32), w4_words[0].bitcast(I32))
-        nc.sync.dma_start(w8_late[:], w8_by_partition[:, :, HALF : HALF + QUARTER])
-        nc.sync.dma_start(w8_last[:], w8_by_partition[:, :, HALF + QUARTER : M])
+        nc.sync.dma_start(w8_late[:], w8_by_partition[:, :, HALF:M])
 
         window_lines = ts_window[:].rearrange("q (p c) -> q p c", p=P)
         for g in range(T // BANK):
-            spread = psum.tile([P, BANK], F32, name="bank%d" % g)
+            spread = bank(g)
             for i in range(LINE):
                 c = LINE * g + i
                 nc.tensor.transpose(
@@ -132,32 +158,28 @@ def tile_list_tabts_bias_kernel(
                 window_lines[:, :, LINE * g : LINE * (g + 1)], spread[:].rearrange("q (i p) -> q p i", i=LINE)
             )
 
-        bias_bank = psum.tile([P, BANK], F32, name="bank7")
+        bias_bank = bank(BANKS - 1)
         nc.tensor.transpose(bias_bank[:, 0:P], bias_rows[:], identity[:])
 
-        def list_slice(s):
-            return offsets[:, s * LIST_COLS : (s + 1) * LIST_COLS]
+        def list_slices(first, count):
+            return offsets[:, first * LIST_COLS : (first + count) * LIST_COLS]
 
         def gather_words1(s, tile):
             picked_words1[s] = tile
-            nc.vector.tensor_copy(tile[:], words1_window[:].bitcast(U32).indirect(list_slice(s)))
+            nc.vector.tensor_copy(tile[:], words1_window[:].bitcast(U32).indirect(list_slices(s, 1)))
 
         def gather_ts(first, count, tile):
-            for s in range(count):
-                picked_ts[first + s] = tile[:, s * BANK : (s + 1) * BANK]
-            nc.vector.tensor_copy(
-                tile[:], ts_window[:].indirect(offsets[:, first * LIST_COLS : (first + count) * LIST_COLS])
-            )
+            for i in range(count):
+                picked_ts[first + i] = tile[:, i * BANK : (i + 1) * BANK]
+            nc.vector.tensor_copy(tile[:], ts_window[:].indirect(list_slices(first, count)))
 
         def round_w8(q):
-            raw = (w8_early[:, :, 0:QUARTER], w8_early[:, :, QUARTER:HALF], w8_late[:], w8_last[:])[q]
-            if q < 2:
-                w8_bf16[q] = shared_tile(W8_BF16_AT + 2 * KIB * q, [P, QUARTER, PACK], BF16, "w8_bf16_%d" % q)
-            else:
-                w8_bf16[q] = shared_tile(HELD_AT + 2 * KIB * (q - 1), [P, QUARTER, PACK], BF16, "w8_bf16_%d" % q)
+            late, part = divmod(q, 2)
+            raw = (w8_late if late else w8_early)[:, :, part * QUARTER : (part + 1) * QUARTER]
+            offset = (LATE_BF16_AT if late else EARLY_BF16_AT) + part * TILE_BYTES
+            w8_bf16[q] = shared_tile(offset, [P, QUARTER, PACK], BF16, "w8_bf16_%d" % q)
             nc.scalar.copy(
-                w8_bf16[q][:].rearrange("p (c u) i -> p c i u", u=LINE),
-                raw.rearrange("p i (c u) -> p c i u", u=LINE),
+                w8_bf16[q][:].rearrange("p (c u) i -> p c i u", u=LINE), raw.rearrange("p i (c u) -> p c i u", u=LINE)
             )
 
         def quantize_w8(q):
@@ -167,80 +189,87 @@ def tile_list_tabts_bias_kernel(
                 in_=w8_bf16[q][:].rearrange("p n i -> p (n i)"),
             )
 
-        def output_tile(t):
-            s, c = TILES[t]
+        def multiply(acc, s, c):
             rows = slice(c * P, (c + 1) * P)
             entries = slice(s * BANK, (s + 1) * BANK)
             q, first = divmod(c * P, QUARTER)
-            acc = psum.tile([P, BANK], F32, name="bank%d" % (t % 8))
-            nc.tensor.matmul_mx(
-                out=acc[:],
-                lhsT=w8_codes[q][:, first : first + P].bitcast(FP8X4),
-                lhsT_scale=w8_plane[:, rows],
-                rhs=picked_words0[:, entries].bitcast(FP8X4),
-                rhs_scale=picked_scales[:].bitcast(U8)[PLANE0:P, entries],
-                start=True,
-                stop=False,
-            )
-            nc.tensor.matmul_mx(
-                out=acc[:],
-                lhsT=w4_codes[:, 2 * c * P : 2 * (c + 1) * P].bitcast(FP4X4),
-                lhsT_scale=w4_plane[:].bitcast(U8)[:, rows],
-                rhs=picked_words1[s][:].bitcast(FP8X4),
-                rhs_scale=picked_scales[:].bitcast(U8)[:, entries],
-                start=False,
-                stop=True,
-            )
+            planes = table_planes[:].bitcast(U8)
+            passes = [
+                (
+                    w8_codes[q][:, first : first + P].bitcast(FP8X4),
+                    w8_plane[:, rows],
+                    picked_words0[:, entries],
+                    planes[PLANE0:P, entries],
+                ),
+                (
+                    w4_codes[:, 2 * c * P : 2 * (c + 1) * P].bitcast(FP4X4),
+                    w4_plane[:].bitcast(U8)[:, rows],
+                    picked_words1[s][:],
+                    planes[:, entries],
+                ),
+            ]
+            if c >= EARLY_ROWS:
+                passes = passes[::-1]
+            for i, (weights, weight_plane, words, word_plane) in enumerate(passes):
+                nc.tensor.matmul_mx(
+                    out=acc[:],
+                    lhsT=weights,
+                    lhsT_scale=weight_plane,
+                    rhs=words.bitcast(FP8X4),
+                    rhs_scale=word_plane,
+                    start=i == 0,
+                    stop=i == len(passes) - 1,
+                )
+
+        def output_tile(t):
+            s, c = order[t]
+            result = results[c][:, s * BANK : (s + 1) * BANK]
             bias_column = bias[:, c : c + 1]
+            acc = bank(t)
+            multiply(acc, s, c)
             if (s, c) in POOL_TILES:
-                scaled = ring.tile([P, BANK], F32, name="scaled_pool")
-                if t < 4:
-                    plain = shared_tile(HELD_AT + (2 + t) * KIB, [P, BANK], F32, "plain_first%d" % t)
+                if c < EARLY_ROWS:
+                    plain = shared_tile(LATE_BF16_AT + c // 2 * TILE_BYTES, [P, BANK], F32, "plain_early%d" % c)
                 else:
-                    plain = ring.tile([P, BANK], F32, name="plain", bufs=2)
+                    plain = ring.tile([P, BANK], F32, name="plain", bufs=PLAIN_BUFS)
+                product = ring.tile([P, BANK], F32, name="pool_product")
                 nc.scalar.copy(plain[:], acc[:])
-                nc.gpsimd.tensor_tensor(scaled[:], plain[:], picked_ts[s], MULT)
-                nc.gpsimd.tensor_scalar(results[c][:, entries], scaled[:], 1.0, bias_column, MULT, ADD)
+                nc.gpsimd.tensor_tensor(product[:], plain[:], picked_ts[s], MULT)
+                nc.gpsimd.tensor_scalar(result, product[:], 1.0, bias_column, MULT, ADD)
                 return
             if (s, c) == (0, 1):
-                scaled = shared_tile(HELD_AT, [P, BANK], F32, "scaled_held")
+                scaled = shared_tile(FIRST_SCALED_AT, [P, BANK], F32, "first_scaled")
             else:
                 scaled = ring.tile([P, BANK], F32, name="scaled", bufs=SCALED_BUFS)
-            last = t == len(TILES) - 1
-            width = BANK // (LAST_TILE_PIECES if last else 1)
-            for start in range(0, BANK, width):
-                part = slice(start, start + width)
-                cols = slice(s * BANK + start, s * BANK + start + width)
-                nc.vector.tensor_tensor(scaled[:, part], acc[:, part], picked_ts[s][:, part], MULT)
-                if (s, c) in POOL_BIAS:
-                    nc.gpsimd.tensor_scalar(results[c][:, cols], scaled[:, part], 1.0, bias_column, MULT, ADD)
-                else:
-                    nc.scalar.activation(results[c][:, cols], scaled[:, part], IDENTITY, bias=bias_column)
-                if last:
-                    nc.sync.dma_start(out[rows, cols], results[c][:, cols])
-            if (s, c) in STORE_FROM:
-                cols = slice(STORE_FROM[(s, c)] * BANK, (s + 1) * BANK)
-                nc.sync.dma_start(out[rows, cols], results[c][:, cols])
+            nc.vector.tensor_tensor(scaled[:], acc[:], picked_ts[s], MULT)
+            if (s, c) in POOL_BIASES:
+                nc.gpsimd.tensor_scalar(result, scaled[:], 1.0, bias_column, MULT, ADD)
+            else:
+                nc.scalar.activation(result, scaled[:], IDENTITY, bias=bias_column)
+            first = first_stored_slice(s, c)
+            if first is not None:
+                cols = slice(first * BANK, (s + 1) * BANK)
+                nc.sync.dma_start(out[c * P : (c + 1) * P, cols], results[c][:, cols])
 
         picked_words0 = keep.tile([P, S], U32, name="picked_words0", align_bytes=64)
         nc.vector.tensor_copy(picked_words0[:], words0_window[:].bitcast(U32).indirect(offsets[:]))
         round_w8(0)
         round_w8(1)
-        bias = shared_tile(W8_EARLY_AT + 7 * KIB, [P, ROW_TILES], F32, "bias")
+        bias = shared_tile(BIAS_AT, [P, ROW_TILES], F32, "bias")
         nc.scalar.copy(bias[:], bias_bank[:, 0:ROW_TILES])
-        gather_ts(0, 1, keep.tile([P, BANK], F32, name="picked_ts0", align_bytes=64))
+        gather_ts(0, 1, shared_tile(PICKED_TS0_AT, [P, BANK], F32, "picked_ts0"))
         quantize_w8(0)
         quantize_w8(1)
         gather_ts(1, 2, shared_tile(W8_EARLY_AT, [P, 2 * BANK], F32, "picked_ts12"))
-        for s in range(2):
+        for s in range(SLICES - 1):
             gather_words1(s, keep.tile([P, BANK], U32, name="picked_words1_%d" % s, align_bytes=64))
-        for t in range(len(TILES)):
-            if t == 6:
+        for t, (s, c) in enumerate(order):
+            if t == LAST_GATHER_AT:
                 round_w8(2)
-                gather_words1(2, shared_tile(HELD_AT, [P, BANK], U32, "picked_words1_2"))
-            if t == 8:
+                gather_words1(SLICES - 1, shared_tile(FIRST_SCALED_AT, [P, BANK], U32, "picked_words1_last"))
+            if (s, c) == (0, EARLY_ROWS):
                 round_w8(3)
                 quantize_w8(2)
-            if t == 13:
+            if (s, c) == (0, EARLY_ROWS + 2):
                 quantize_w8(3)
             output_tile(t)

@@ -37,7 +37,7 @@ SCALE_RUNS = ((0, 4, 16), (4, 32, -8), (36, 32, -4), (68, 32, 0), (108, 4, 12))
 
 POOL_TILES = [(0, c) for c in range(0, ROW_TILES, 2)]
 POOL_LEAD = 5
-POOL_BIASES = [(1, EARLY_ROWS - 1), (2, 0), (2, 1)]
+POOL_BIASES = [(1, 3), (2, 0), (2, 1), (1, 5), (2, 7)]
 LAST_GATHER_AT = 6
 SCALED_BUFS = 16
 PLAIN_BUFS = 2
@@ -60,13 +60,8 @@ LATE_BF16_AT = 44 * KIB
 
 
 def tile_order():
-    order = [(s, c) for s in range(SLICES) for c in range(EARLY_ROWS)]
-    for even in range(EARLY_ROWS, ROW_TILES, 2):
-        odd = even + 1
-        order = order + [(0, odd), (1, even), (1, odd), (2, odd), (2, even)]
-        at = order.index((1, even)) - POOL_LEAD
-        order = order[:at] + [(0, even)] + order[at:]
-    return order
+    return [(0, 0), (0, 1), (0, 2), (0, 3), (1, 0), (1, 1), (1, 2), (1, 3), (0, 4), (2, 0), (2, 1), (2, 2), (2, 3),
+            (0, 5), (1, 4), (1, 5), (0, 6), (2, 5), (2, 4), (0, 7), (1, 6), (1, 7), (2, 7), (2, 6)]
 
 
 def first_stored_slice(s, c):
@@ -232,13 +227,18 @@ def tile_list_tabts_bias_kernel(
                     plain = shared_tile(LATE_BF16_AT + c // 2 * TILE_BYTES, [P, BANK], F32, "plain_early%d" % c)
                 else:
                     plain = ring.tile([P, BANK], F32, name="plain", bufs=PLAIN_BUFS)
-                product = ring.tile([P, BANK], F32, name="pool_product")
+                if c == 6:
+                    product = shared_tile(48 * KIB, [P, BANK], F32, "last_product")
+                else:
+                    product = ring.tile([P, BANK], F32, name="pool_product")
                 nc.scalar.copy(plain[:], acc[:])
                 nc.gpsimd.tensor_tensor(product[:], plain[:], picked_ts[s], MULT)
                 nc.gpsimd.tensor_scalar(result, product[:], 1.0, bias_column, MULT, ADD)
                 return
             if (s, c) == (0, 1):
                 scaled = shared_tile(FIRST_SCALED_AT, [P, BANK], F32, "first_scaled")
+            elif (s, c) == (1, 5):
+                scaled = shared_tile(48 * KIB, [P, BANK], F32, "held_scaled")
             else:
                 scaled = ring.tile([P, BANK], F32, name="scaled", bufs=SCALED_BUFS)
             nc.vector.tensor_tensor(scaled[:], acc[:], picked_ts[s], MULT)
@@ -270,6 +270,6 @@ def tile_list_tabts_bias_kernel(
             if (s, c) == (0, EARLY_ROWS):
                 round_w8(3)
                 quantize_w8(2)
-            if (s, c) == (0, EARLY_ROWS + 2):
+            if (s, c) == (1, EARLY_ROWS + 1):
                 quantize_w8(3)
             output_tile(t)

@@ -48,9 +48,7 @@ TILE_BYTES = 4 * BANK
 WORDS1_AT = 0
 SCALE_WINDOW_AT = 16 * KIB - OVERLAP
 W4_CODES_AT = 16 * KIB
-PICKED_TS0_AT = 20 * KIB
-W8_LATE_AT = 22 * KIB
-PICKED_ROWS_AT = W8_LATE_AT - S // 2
+W8_LATE_AT = 20 * KIB - 2 * OVERLAP
 W8_EARLY_AT = 30 * KIB
 BIAS_AT = W8_EARLY_AT + 2 * TILE_BYTES
 EARLY_BF16_AT = 38 * KIB
@@ -126,18 +124,23 @@ def tile_list_tabts_bias_kernel(
         nc.sync.dma_start(words0_window[:], table_words(0))
         nc.sync.dma_start(w8_early[:], w8_by_partition[:, :, 0:HALF])
 
-        picked_rows = shared_tile(PICKED_ROWS_AT, [P, S], U8, "picked_rows")
+        picked_rows = keep.tile([P, S], U8, name="picked_rows", align_bytes=64)
         nc.vector.tensor_copy(picked_rows[:], scale_window[:].bitcast(U8).indirect(offsets[:]))
-        for partition, count, row in SCALE_RUNS:
+
+        def deal(partition, count, row):
             nc.sync.dma_start(
                 table_planes[partition : partition + count, :],
                 picked_rows[:].bitcast(I32)[SCALE_ROW0 + row : SCALE_ROW0 + row + count, :],
             )
 
+        for run in SCALE_RUNS[1:]:
+            deal(*run)
+
         words1_window = shared_tile(WORDS1_AT, [P, T], I32, "words1_window")
         w4_codes = shared_tile(W4_CODES_AT, [P, 2 * M], U8, "w4_codes")
         w8_late = shared_tile(W8_LATE_AT, [P, PACK, HALF], F32, "w8_late")
         nc.sync.dma_start(words1_window[:], table_words(1))
+        deal(*SCALE_RUNS[0])
         nc.sync.dma_start(w4_codes[:].bitcast(I32), w4_words[0].bitcast(I32))
         nc.sync.dma_start(w8_late[:], w8_by_partition[:, :, HALF:M])
 
@@ -257,7 +260,7 @@ def tile_list_tabts_bias_kernel(
         round_w8(1)
         bias = shared_tile(BIAS_AT, [P, ROW_TILES], F32, "bias")
         nc.scalar.copy(bias[:], bias_bank[:, 0:ROW_TILES])
-        gather_ts(0, 1, shared_tile(PICKED_TS0_AT, [P, BANK], F32, "picked_ts0"))
+        gather_ts(0, 1, keep.tile([P, BANK], F32, name="picked_ts0", align_bytes=64))
         quantize_w8(0)
         quantize_w8(1)
         gather_ts(1, 2, shared_tile(W8_EARLY_AT, [P, 2 * BANK], F32, "picked_ts12"))

@@ -36,9 +36,10 @@ PLANE0 = 12
 SCALE_RUNS = ((0, 4, 16), (4, 32, -8), (36, 32, -4), (68, 32, 0), (108, 4, 12))
 
 POOL_TILES = [(0, c) for c in range(0, ROW_TILES, 2)]
-POOL_LEAD = 5
 POOL_BIASES = [(1, 3), (2, 0), (2, 1), (1, 5), (2, 7)]
 LAST_GATHER_AT = 6
+THIRD_QUANTISE_AT = (0, EARLY_ROWS)
+LAST_QUANTISE_AT = (1, EARLY_ROWS + 1)
 SCALED_BUFS = 16
 PLAIN_BUFS = 2
 
@@ -55,11 +56,20 @@ EARLY_BF16_AT = 38 * KIB
 TS_COLS_AT = EARLY_BF16_AT + TILE_BYTES - OVERLAP
 FIRST_SCALED_AT = 42 * KIB
 LATE_BF16_AT = 44 * KIB
+LAST_PRODUCT_AT = 48 * KIB
 
 
 def tile_order():
-    return [(0, 0), (0, 1), (0, 2), (0, 3), (1, 0), (1, 1), (1, 2), (1, 3), (0, 4), (2, 0), (2, 1), (2, 2), (2, 3),
-            (0, 5), (1, 4), (1, 5), (0, 6), (2, 5), (2, 4), (0, 7), (1, 6), (1, 7), (2, 7), (2, 6)]
+    early = range(EARLY_ROWS)
+    order = [(s, c) for s in range(SLICES - 1) for c in early]
+    order.append(THIRD_QUANTISE_AT)
+    order.extend((SLICES - 1, c) for c in early)
+    for c in range(EARLY_ROWS, ROW_TILES, 2):
+        for tile in [(0, c + 1), (1, c), (1, c + 1), (2, c + 1), (2, c)]:
+            order.append(tile)
+            if tile == LAST_QUANTISE_AT:
+                order.append(POOL_TILES[-1])
+    return order
 
 
 def first_stored_slice(s, c):
@@ -101,11 +111,12 @@ def tile_list_tabts_bias_kernel(
         results = [keep.tile([P, S], F32, name="result%d" % c) for c in range(ROW_TILES)]
         w8_bf16, picked_words1, picked_ts = {}, {}, {}
         order = tile_order()
+        vector_tiles = [tile for tile in order if tile not in POOL_TILES]
 
         nc.vector.memset(bias_rows[:], 0.0)
         nc.vector.memset(w4_plane[:], 0)
         nc.vector.memset(scale_window[0:SCALE_ROW0, :], 0)
-        nc.vector.memset(table_planes[:], 0)
+        nc.vector.memset(table_planes[SCALE_ROW0:P, :], 0)
         make_identity(nc, identity[:])
 
         nc.gpsimd.dma_start(bias_rows[0:ROW_TILES, :], b.rearrange("(c x) -> c x", x=P))
@@ -118,8 +129,8 @@ def tile_list_tabts_bias_kernel(
             return tab_words[a].rearrange("p t i -> p (t i)").bitcast(I32)
 
         w8_by_partition = w8.rearrange("(p i) n -> p i n", i=PACK)
-        nc.sync.dma_start(offsets[:], offs)
         nc.sync.dma_start(scale_window[SCALE_ROW0:P, :], tab_scales.rearrange("a q t -> (a q) t").bitcast(I32))
+        nc.sync.dma_start(offsets[:], offs)
         nc.sync.dma_start(ts_cols[:], ts[0].rearrange("(p c) -> p c", p=P))
         nc.sync.dma_start(words0_window[:], table_words(0))
         nc.sync.dma_start(w8_early[:], w8_by_partition[:, :, 0:HALF])
@@ -230,18 +241,18 @@ def tile_list_tabts_bias_kernel(
                     plain = shared_tile(LATE_BF16_AT + c // 2 * TILE_BYTES, [P, BANK], F32, "plain_early%d" % c)
                 else:
                     plain = ring.tile([P, BANK], F32, name="plain", bufs=PLAIN_BUFS)
-                if c == 6:
-                    product = shared_tile(48 * KIB, [P, BANK], F32, "last_product")
+                if (s, c) == POOL_TILES[-1]:
+                    product = shared_tile(LAST_PRODUCT_AT, [P, BANK], F32, "last_product")
                 else:
                     product = ring.tile([P, BANK], F32, name="pool_product")
                 nc.scalar.copy(plain[:], acc[:])
                 nc.gpsimd.tensor_tensor(product[:], plain[:], picked_ts[s], MULT)
                 nc.gpsimd.tensor_scalar(result, product[:], 1.0, bias_column, MULT, ADD)
                 return
-            if (s, c) == (0, 1):
+            if (s, c) == vector_tiles[0]:
                 scaled = shared_tile(FIRST_SCALED_AT, [P, BANK], F32, "first_scaled")
-            elif (s, c) == (1, 5):
-                scaled = shared_tile(48 * KIB, [P, BANK], F32, "held_scaled")
+            elif (s, c) == LAST_QUANTISE_AT:
+                scaled = shared_tile(LAST_PRODUCT_AT, [P, BANK], F32, "held_scaled")
             else:
                 scaled = ring.tile([P, BANK], F32, name="scaled", bufs=SCALED_BUFS)
             nc.vector.tensor_tensor(scaled[:], acc[:], picked_ts[s], MULT)
@@ -270,9 +281,9 @@ def tile_list_tabts_bias_kernel(
             if t == LAST_GATHER_AT:
                 round_w8(2)
                 gather_words1(SLICES - 1, shared_tile(FIRST_SCALED_AT, [P, BANK], U32, "picked_words1_last"))
-            if (s, c) == (0, EARLY_ROWS):
+            if (s, c) == THIRD_QUANTISE_AT:
                 round_w8(3)
                 quantize_w8(2)
-            if (s, c) == (1, EARLY_ROWS + 1):
+            if (s, c) == LAST_QUANTISE_AT:
                 quantize_w8(3)
             output_tile(t)

@@ -49,10 +49,11 @@ TILE_BYTES = 4 * BANK
 WORDS1_AT = 0
 SCALE_WINDOW_AT = 16 * KIB - OVERLAP
 W4_CODES_AT = 16 * KIB
-W8_LATE_AT = 20 * KIB - 2 * OVERLAP
+W4_PLANE_AT = 18 * KIB
 W8_EARLY_AT = 30 * KIB
 BIAS_AT = W8_EARLY_AT + 2 * TILE_BYTES
-EARLY_BF16_AT = 38 * KIB
+EARLY_BF16_AT = 52 * KIB
+W8_LATE_AT = EARLY_BF16_AT + 2 * TILE_BYTES - OVERLAP
 TS_COLS_AT = EARLY_BF16_AT + TILE_BYTES - OVERLAP
 FIRST_SCALED_AT = 42 * KIB
 LATE_BF16_AT = 44 * KIB
@@ -105,7 +106,6 @@ def tile_list_tabts_bias_kernel(
         words0_window = keep.tile([P, T], I32, name="words0_window", align_bytes=64)
         w8_codes = [keep.tile([P, QUARTER], U32, name="w8_codes%d" % q, align_bytes=64) for q in range(4)]
         w8_plane = keep.tile([P, M], U8, name="w8_plane", align_bytes=64)
-        w4_plane = keep.tile([P, M // 4], I32, name="w4_plane", align_bytes=64)
         table_planes = keep.tile([P, S // 4], I32, name="table_planes", align_bytes=64)
         identity = keep.tile([P, P], F32, name="identity")
         results = [keep.tile([P, S], F32, name="result%d" % c) for c in range(ROW_TILES)]
@@ -114,16 +114,11 @@ def tile_list_tabts_bias_kernel(
         vector_tiles = [tile for tile in order if tile not in POOL_TILES]
 
         nc.vector.memset(bias_rows[:], 0.0)
-        nc.vector.memset(w4_plane[:], 0)
         nc.vector.memset(scale_window[0:SCALE_ROW0, :], 0)
         nc.vector.memset(table_planes[SCALE_ROW0:P, :], 0)
         make_identity(nc, identity[:])
 
         nc.gpsimd.dma_start(bias_rows[0:ROW_TILES, :], b.rearrange("(c x) -> c x", x=P))
-        for q in range(P // QUADRANT):
-            nc.gpsimd.dma_start(
-                w4_plane[QUADRANT * q : QUADRANT * q + 4, :], w4_scales[0].bitcast(I32)[4 * q : 4 * q + 4, :]
-            )
 
         def table_words(a):
             return tab_words[a].rearrange("p t i -> p (t i)").bitcast(I32)
@@ -149,11 +144,14 @@ def tile_list_tabts_bias_kernel(
 
         words1_window = shared_tile(WORDS1_AT, [P, T], I32, "words1_window")
         w4_codes = shared_tile(W4_CODES_AT, [P, 2 * M], U8, "w4_codes")
-        w8_late = shared_tile(W8_LATE_AT, [P, PACK, HALF], F32, "w8_late")
         nc.sync.dma_start(words1_window[:], table_words(1))
         deal(*SCALE_RUNS[0])
         nc.sync.dma_start(w4_codes[:].bitcast(I32), w4_words[0].bitcast(I32))
-        nc.sync.dma_start(w8_late[:], w8_by_partition[:, :, HALF:M])
+        w4_plane = shared_tile(W4_PLANE_AT, [P, M // 4], I32, "w4_plane")
+        for q in range(P // QUADRANT):
+            nc.gpsimd.dma_start(
+                w4_plane[QUADRANT * q : QUADRANT * q + 4, :], w4_scales[0].bitcast(I32)[4 * q : 4 * q + 4, :]
+            )
 
         window_lines = ts_window[:].rearrange("q (p c) -> q p c", p=P)
         for g in range(T // BANK):
@@ -274,6 +272,8 @@ def tile_list_tabts_bias_kernel(
         gather_ts(0, 1, keep.tile([P, BANK], F32, name="picked_ts0", align_bytes=64))
         quantize_w8(0)
         quantize_w8(1)
+        w8_late = shared_tile(W8_LATE_AT, [P, PACK, HALF], F32, "w8_late")
+        nc.sync.dma_start(w8_late[:], w8_by_partition[:, :, HALF:M])
         gather_ts(1, 2, shared_tile(W8_EARLY_AT, [P, 2 * BANK], F32, "picked_ts12"))
         for s in range(SLICES - 1):
             gather_words1(s, keep.tile([P, BANK], U32, name="picked_words1_%d" % s, align_bytes=64))

@@ -53,7 +53,7 @@ W4_PLANE_AT = 18 * KIB
 W8_EARLY_AT = 30 * KIB
 BIAS_AT = W8_EARLY_AT + 2 * TILE_BYTES
 EARLY_BF16_AT = 52 * KIB
-W8_LATE_AT = EARLY_BF16_AT + 2 * TILE_BYTES - OVERLAP
+TS_WINDOW_AT = 56 * KIB
 TS_COLS_AT = EARLY_BF16_AT + TILE_BYTES - OVERLAP
 FIRST_SCALED_AT = 42 * KIB
 LATE_BF16_AT = 44 * KIB
@@ -102,7 +102,7 @@ def tile_list_tabts_bias_kernel(
         ts_cols = shared_tile(TS_COLS_AT, [P, T // P], F32, "ts_cols")
         w8_early = shared_tile(W8_EARLY_AT, [P, PACK, HALF], F32, "w8_early")
         bias_rows = keep.tile([P, P], F32, name="bias_rows")
-        ts_window = keep.tile([P, T], F32, name="ts_window", align_bytes=64)
+        ts_window = shared_tile(TS_WINDOW_AT, [P, T], F32, "ts_window")
         words0_window = keep.tile([P, T], I32, name="words0_window", align_bytes=64)
         w8_codes = [keep.tile([P, QUARTER], U32, name="w8_codes%d" % q, align_bytes=64) for q in range(4)]
         w8_plane = keep.tile([P, M], U8, name="w8_plane", align_bytes=64)
@@ -272,9 +272,9 @@ def tile_list_tabts_bias_kernel(
         gather_ts(0, 1, keep.tile([P, BANK], F32, name="picked_ts0", align_bytes=64))
         quantize_w8(0)
         quantize_w8(1)
-        w8_late = shared_tile(W8_LATE_AT, [P, PACK, HALF], F32, "w8_late")
-        nc.sync.dma_start(w8_late[:], w8_by_partition[:, :, HALF:M])
         gather_ts(1, 2, shared_tile(W8_EARLY_AT, [P, 2 * BANK], F32, "picked_ts12"))
+        w8_late = shared_tile(TS_WINDOW_AT, [P, PACK, HALF], F32, "w8_late")
+        nc.sync.dma_start(w8_late[:], w8_by_partition[:, :, HALF:M])
         for s in range(SLICES - 1):
             gather_words1(s, keep.tile([P, BANK], U32, name="picked_words1_%d" % s, align_bytes=64))
         for t, (s, c) in enumerate(order):

from contextlib import ExitStack

import concourse.mybir as mybir
from concourse.masks import make_identity

K, M, T, S = 1024, 1024, 4096, 1536
FLOPS = 2 * K * M * S

F32 = mybir.dt.float32
BF16 = mybir.dt.bfloat16
I32 = mybir.dt.int32
U32 = mybir.dt.uint32
U16 = mybir.dt.uint16
U8 = mybir.dt.uint8
FP8X4 = mybir.dt.float8_e4m3fn_x4
FP4X4 = mybir.dt.float4_e2m1fn_x4
MULT = mybir.AluOpType.mult
ADD = mybir.AluOpType.add
IDENTITY = mybir.ActivationFunctionType.Identity

P = 128
PACK = 4
BANK = 512
BANKS = 8
SLICES = S // BANK
LIST_COLS = BANK // 16
HALF = M // 2
QUARTER = M // 4
ROW_TILES = M // P
EARLY_ROWS = ROW_TILES // 2
LINE = 4
QUADRANT = 32

SCALE_ROW0 = P - QUADRANT
PLANE0 = 12
SCALE_RUNS = ((0, 4, 16), (4, 32, -8), (36, 32, -4), (68, 32, 0), (108, 4, 12))

POOL_TILES = [(0, c) for c in range(0, ROW_TILES, 2)]
POOL_BIASES = [(1, 3), (2, 0), (2, 1), (1, 5), (2, 7)]
LAST_GATHER_AT = 6
THIRD_QUANTISE_AT = (0, EARLY_ROWS)
LAST_QUANTISE_AT = (1, EARLY_ROWS + 1)
SCALED_BUFS = 16
PLAIN_BUFS = 2

KIB = 1024
OVERLAP = 64
TILE_BYTES = 4 * BANK
WORDS1_AT = 0
SCALE_WINDOW_AT = 16 * KIB - OVERLAP
W4_CODES_AT = 16 * KIB
W4_PLANE_AT = 18 * KIB
W8_EARLY_AT = 30 * KIB
BIAS_AT = W8_EARLY_AT + 2 * TILE_BYTES
EARLY_BF16_AT = 52 * KIB
TS_WINDOW_AT = 56 * KIB
TS_COLS_AT = EARLY_BF16_AT + TILE_BYTES - OVERLAP
FIRST_SCALED_AT = 42 * KIB
LATE_BF16_AT = 44 * KIB
LAST_PRODUCT_AT = 48 * KIB


def tile_order():
    early = range(EARLY_ROWS)
    order = [(s, c) for s in range(SLICES - 1) for c in early]
    order.append(THIRD_QUANTISE_AT)
    order.extend((SLICES - 1, c) for c in early)
    for c in range(EARLY_ROWS, ROW_TILES, 2):
        for tile in [(0, c + 1), (1, c), (1, c + 1), (2, c + 1), (2, c)]:
            order.append(tile)
            if tile == LAST_QUANTISE_AT:
                order.append(POOL_TILES[-1])
    return order


def first_stored_slice(s, c):
    if s == 1 and (0, c) in POOL_TILES:
        return 0
    if c >= EARLY_ROWS and (0, c) not in POOL_TILES and s > 0:
        return 1 if s == 2 else None
    return s


def tile_list_tabts_bias_kernel(
    tc, tab_words, tab_scales, w8, w4_words, w4_scales, ts, b, offs, out
):
    nc = tc.nc
    with ExitStack() as ctx:
        keep = ctx.enter_context(tc.tile_pool(name="keep", bufs=1))
        ring = ctx.enter_context(tc.tile_pool(name="ring", bufs=1))
        shared = ctx.enter_context(tc.tile_pool(name="shared", bufs=1))
        psum = ctx.enter_context(tc.psum_pool(name="psum", bufs=1))

        def shared_tile(offset, shape, dtype, name):
            return shared.tile(shape, dtype, name=name, offset=offset, align_bytes=64)

        def bank(i):
            return psum.tile([P, BANK], F32, name="bank%d" % (i % BANKS))

        offsets = keep.tile([P, S // 16], U16, name="offsets")
        scale_window = shared_tile(SCALE_WINDOW_AT, [P, T // 4], I32, "scale_window")
        ts_cols = shared_tile(TS_COLS_AT, [P, T // P], F32, "ts_cols")
        w8_early = shared_tile(W8_EARLY_AT, [P, PACK, HALF], F32, "w8_early")
        bias_rows = keep.tile([P, P], F32, name="bias_rows")
        ts_window = shared_tile(TS_WINDOW_AT, [P, T], F32, "ts_window")
        words0_window = keep.tile([P, T], I32, name="words0_window", align_bytes=64)
        w8_codes = [keep.tile([P, QUARTER], U32, name="w8_codes%d" % q, align_bytes=64) for q in range(4)]
        w8_plane = keep.tile([P, M], U8, name="w8_plane", align_bytes=64)
        table_planes = keep.tile([P, S // 4], I32, name="table_planes", align_bytes=64)
        identity = keep.tile([P, P], F32, name="identity")
        results = [keep.tile([P, S], F32, name="result%d" % c) for c in range(ROW_TILES)]
        w8_bf16, picked_words1, picked_ts = {}, {}, {}
        order = tile_order()
        vector_tiles = [tile for tile in order if tile not in POOL_TILES]

        nc.vector.memset(bias_rows[:], 0.0)
        nc.vector.memset(scale_window[0:SCALE_ROW0, :], 0)
        nc.vector.memset(table_planes[SCALE_ROW0:P, :], 0)
        make_identity(nc, identity[:])

        nc.gpsimd.dma_start(bias_rows[0:ROW_TILES, :], b.rearrange("(c x) -> c x", x=P))

        def table_words(a):
            return tab_words[a].rearrange("p t i -> p (t i)").bitcast(I32)

        w8_by_partition = w8.rearrange("(p i) n -> p i n", i=PACK)
        nc.sync.dma_start(scale_window[SCALE_ROW0:P, :], tab_scales.rearrange("a q t -> (a q) t").bitcast(I32))
        nc.sync.dma_start(offsets[:], offs)
        nc.sync.dma_start(ts_cols[:], ts[0].rearrange("(p c) -> p c", p=P))
        nc.sync.dma_start(words0_window[:], table_words(0))
        nc.sync.dma_start(w8_early[:], w8_by_partition[:, :, 0:HALF])

        picked_rows = keep.tile([P, S], U8, name="picked_rows", align_bytes=64)
        nc.vector.tensor_copy(picked_rows[:], scale_window[:].bitcast(U8).indirect(offsets[:]))

        def deal(partition, count, row):
            nc.sync.dma_start(
                table_planes[partition : partition + count, :],
                picked_rows[:].bitcast(I32)[SCALE_ROW0 + row : SCALE_ROW0 + row + count, :],
            )

        for run in SCALE_RUNS[1:]:
            deal(*run)

        words1_window = shared_tile(WORDS1_AT, [P, T], I32, "words1_window")
        w4_codes = shared_tile(W4_CODES_AT, [P, 2 * M], U8, "w4_codes")
        nc.sync.dma_start(words1_window[:], table_words(1))
        deal(*SCALE_RUNS[0])
        nc.sync.dma_start(w4_codes[:].bitcast(I32), w4_words[0].bitcast(I32))
        w4_plane = shared_tile(W4_PLANE_AT, [P, M // 4], I32, "w4_plane")
        for q in range(P // QUADRANT):
            nc.gpsimd.dma_start(
                w4_plane[QUADRANT * q : QUADRANT * q + 4, :], w4_scales[0].bitcast(I32)[4 * q : 4 * q + 4, :]
            )

        window_lines = ts_window[:].rearrange("q (p c) -> q p c", p=P)
        for g in range(T // BANK):
            spread = bank(g)
            for i in range(LINE):
                c = LINE * g + i
                nc.tensor.transpose(
                    spread[:, i * P : (i + 1) * P], ts_cols[:, c : c + 1].to_broadcast([P, P]), identity[:]
                )
            nc.scalar.copy(
                window_lines[:, :, LINE * g : LINE * (g + 1)], spread[:].rearrange("q (i p) -> q p i", i=LINE)
            )

        bias_bank = bank(BANKS - 1)
        nc.tensor.transpose(bias_bank[:, 0:P], bias_rows[:], identity[:])

        def list_slices(first, count):
            return offsets[:, first * LIST_COLS : (first + count) * LIST_COLS]

        def gather_words1(s, tile):
            picked_words1[s] = tile
            nc.vector.tensor_copy(tile[:], words1_window[:].bitcast(U32).indirect(list_slices(s, 1)))

        def gather_ts(first, count, tile):
            for i in range(count):
                picked_ts[first + i] = tile[:, i * BANK : (i + 1) * BANK]
            nc.vector.tensor_copy(tile[:], ts_window[:].indirect(list_slices(first, count)))

        def round_w8(q):
            late, part = divmod(q, 2)
            raw = (w8_late if late else w8_early)[:, :, part * QUARTER : (part + 1) * QUARTER]
            offset = (LATE_BF16_AT if late else EARLY_BF16_AT) + part * TILE_BYTES
            w8_bf16[q] = shared_tile(offset, [P, QUARTER, PACK], BF16, "w8_bf16_%d" % q)
            nc.scalar.copy(
                w8_bf16[q][:].rearrange("p (c u) i -> p c i u", u=LINE), raw.rearrange("p i (c u) -> p c i u", u=LINE)
            )

        def quantize_w8(q):
            nc.vector.quantize_mx(
                out=w8_codes[q][:].bitcast(FP8X4),
                scales=w8_plane[:, q * QUARTER : (q + 1) * QUARTER],
                in_=w8_bf16[q][:].rearrange("p n i -> p (n i)"),
            )

        def multiply(acc, s, c):
            rows = slice(c * P, (c + 1) * P)
            entries = slice(s * BANK, (s + 1) * BANK)
            q, first = divmod(c * P, QUARTER)
            planes = table_planes[:].bitcast(U8)
            passes = [
                (
                    w8_codes[q][:, first : first + P].bitcast(FP8X4),
                    w8_plane[:, rows],
                    picked_words0[:, entries],
                    planes[PLANE0:P, entries],
                ),
                (
                    w4_codes[:, 2 * c * P : 2 * (c + 1) * P].bitcast(FP4X4),
                    w4_plane[:].bitcast(U8)[:, rows],
                    picked_words1[s][:],
                    planes[:, entries],
                ),
            ]
            if c >= EARLY_ROWS:
                passes = passes[::-1]
            for i, (weights, weight_plane, words, word_plane) in enumerate(passes):
                nc.tensor.matmul_mx(
                    out=acc[:],
                    lhsT=weights,
                    lhsT_scale=weight_plane,
                    rhs=words.bitcast(FP8X4),
                    rhs_scale=word_plane,
                    start=i == 0,
                    stop=i == len(passes) - 1,
                )

        def output_tile(t):
            s, c = order[t]
            result = results[c][:, s * BANK : (s + 1) * BANK]
            bias_column = bias[:, c : c + 1]
            acc = bank(t)
            multiply(acc, s, c)
            if (s, c) in POOL_TILES:
                if c < EARLY_ROWS:
                    plain = shared_tile(LATE_BF16_AT + c // 2 * TILE_BYTES, [P, BANK], F32, "plain_early%d" % c)
                else:
                    plain = ring.tile([P, BANK], F32, name="plain", bufs=PLAIN_BUFS)
                if (s, c) == POOL_TILES[-1]:
                    product = shared_tile(LAST_PRODUCT_AT, [P, BANK], F32, "last_product")
                else:
                    product = ring.tile([P, BANK], F32, name="pool_product")
                nc.scalar.copy(plain[:], acc[:])
                nc.gpsimd.tensor_tensor(product[:], plain[:], picked_ts[s], MULT)
                nc.gpsimd.tensor_scalar(result, product[:], 1.0, bias_column, MULT, ADD)
                return
            if (s, c) == vector_tiles[0]:
                scaled = shared_tile(FIRST_SCALED_AT, [P, BANK], F32, "first_scaled")
            elif (s, c) == LAST_QUANTISE_AT:
                scaled = shared_tile(LAST_PRODUCT_AT, [P, BANK], F32, "held_scaled")
            else:
                scaled = ring.tile([P, BANK], F32, name="scaled", bufs=SCALED_BUFS)
            nc.vector.tensor_tensor(scaled[:], acc[:], picked_ts[s], MULT)
            if (s, c) in POOL_BIASES:
                nc.gpsimd.tensor_scalar(result, scaled[:], 1.0, bias_column, MULT, ADD)
            else:
                nc.scalar.activation(result, scaled[:], IDENTITY, bias=bias_column)
            first = first_stored_slice(s, c)
            if first is not None:
                cols = slice(first * BANK, (s + 1) * BANK)
                nc.sync.dma_start(out[c * P : (c + 1) * P, cols], results[c][:, cols])

        picked_words0 = keep.tile([P, S], U32, name="picked_words0", align_bytes=64)
        nc.vector.tensor_copy(picked_words0[:], words0_window[:].bitcast(U32).indirect(offsets[:]))
        round_w8(0)
        round_w8(1)
        bias = shared_tile(BIAS_AT, [P, ROW_TILES], F32, "bias")
        nc.scalar.copy(bias[:], bias_bank[:, 0:ROW_TILES])
        gather_ts(0, 1, keep.tile([P, BANK], F32, name="picked_ts0", align_bytes=64))
        quantize_w8(0)
        quantize_w8(1)
        gather_ts(1, 2, shared_tile(W8_EARLY_AT, [P, 2 * BANK], F32, "picked_ts12"))
        w8_late = shared_tile(TS_WINDOW_AT, [P, PACK, HALF], F32, "w8_late")
        nc.sync.dma_start(w8_late[:], w8_by_partition[:, :, HALF:M])
        for s in range(SLICES - 1):
            gather_words1(s, keep.tile([P, BANK], U32, name="picked_words1_%d" % s, align_bytes=64))
        for t, (s, c) in enumerate(order):
            if t == LAST_GATHER_AT:
                round_w8(2)
                gather_words1(SLICES - 1, shared_tile(FIRST_SCALED_AT, [P, BANK], U32, "picked_words1_last"))
            if (s, c) == THIRD_QUANTISE_AT:
                round_w8(3)
                quantize_w8(2)
            if (s, c) == LAST_QUANTISE_AT:
                quantize_w8(3)
            output_tile(t)
